import numpy as np
import ml_dtypes


def mxq(x, axis, fmt="e4m3"):
    dtype, down = {"e4m3": (ml_dtypes.float8_e4m3fn, 7), "e5m2": (ml_dtypes.float8_e5m2, 14)}[fmt]
    v = np.moveaxis(np.asarray(x, np.float32).astype(ml_dtypes.bfloat16).astype(np.float64), axis, -1)
    blocks = v.reshape(v.shape[:-1] + (-1, 32))
    amax = np.abs(blocks).max(-1, keepdims=True)
    byte = np.maximum(np.where(amax > 0, np.frexp(amax)[1] - 1 + 127, 0) - down, 1)
    scale = np.exp2(byte - 127.0)
    codes = (blocks / scale).astype(np.float32).astype(dtype).astype(np.float64)
    return np.moveaxis((codes * scale).reshape(v.shape), -1, axis)


WIDE = False


def mx_kscale(k):
    if not WIDE:
        return np.ones(k)
    levels = np.array([10, -10, 5, -5, 0])
    if k % 512:
        return np.exp2(np.random.permutation(np.resize(levels, k // 32))).repeat(32)
    a = np.empty((k // 512, 16))
    for p in range(k // 512):
        a[p, :8] = np.random.permutation(np.resize(levels, 8))
        for g in range(8):
            far = levels[np.abs(levels - a[p, g]) >= 10]
            a[p, g + 8] = far[np.random.randint(len(far))]
    return np.exp2(a.ravel()).repeat(32)


def f64(x):
    return np.asarray(x).astype(np.float64)


def striped(idx):
    return np.tile(idx.reshape(-1, 16).T, (8, 1)).astype(np.uint16)


def unstriped(offs):
    return offs[:16].T.reshape(-1).astype(np.int64)


def pack_weight(w):
    k, n = w.shape
    w = f64(np.asarray(w, np.float32).astype(ml_dtypes.bfloat16)).reshape(k // 32, 32, n)
    amax = np.abs(w).max(1)
    byte = np.clip(np.where(amax > 0, np.frexp(amax)[1] - 1 + 127 - 7, 1), 1, 254)
    scaled = (w * np.exp2(127.0 - byte)[:, None, :]).reshape(k, n).astype(np.float32)
    words = np.ascontiguousarray(scaled.reshape(k // 512, 128, 4, n).transpose(0, 1, 3, 2)).astype(ml_dtypes.float8_e4m3fn).view(np.uint8)
    return words, np.ascontiguousarray(byte.astype(np.uint8).reshape(k // 512, 16, n))


def unpack_weight(words, scales):
    g, p, n, _ = words.shape
    vals = np.ascontiguousarray(words).view(ml_dtypes.float8_e4m3fn).astype(np.float64) * np.repeat(np.exp2(scales.astype(np.float64) - 127.0), 8, axis=1)[..., None]
    return vals.transpose(0, 1, 3, 2).reshape(g * 512, n)


def relu(v):
    return np.maximum(v, 0.0)

def planes(y):
    n, m = y.shape
    v = y.astype(np.float32).astype(ml_dtypes.bfloat16).astype(np.float64).reshape(n // 32, 32, m)
    top = np.abs(v).max(1)
    byte = np.clip(np.where(top > 0, np.frexp(top)[1] - 1 + 127 - 7, 1), 1, 254)
    codes = (v * np.exp2(127.0 - byte)[:, None, :]).reshape(n, m).astype(np.float32).astype(ml_dtypes.float8_e4m3fn).view(np.uint8)
    words = codes.reshape(n // 512, 128, 4, m).transpose(0, 1, 3, 2)
    return np.ascontiguousarray(words), np.ascontiguousarray(byte.astype(np.uint8).reshape(n // 512, 16, m))


K, T, S, V, H = 512, 1024, 512, 256, 512


def setup_inputs():
    n = np.random.standard_normal
    s = mx_kscale(K)[:, None]
    u = mx_kscale(H)
    packed_xT = pack_weight(n((K, T)) * s)
    packed_w2 = pack_weight(n((H, H)) / np.sqrt(2 * H) / u[:, None])
    packed_w3 = pack_weight(n((H, H)) / np.sqrt(2 * H) / u[:, None])
    return {
        "x_words": packed_xT[0],
        "x_scales": packed_xT[1],
        "w1": (n((K, H)) / np.sqrt(K) / s * u).astype(np.float32),
        "w2_words": packed_w2[0],
        "w2_scales": packed_w2[1],
        "w3_words": packed_w3[0],
        "w3_scales": packed_w3[1],
        "offs": striped(np.random.permutation(T)[:S]),
        "cen": striped(np.random.permutation(S)[:V]),
        "pos1": striped(np.random.permutation(S)[:V]),
        "pos2": striped(np.random.permutation(S)[:V]),
        "pos3": striped(np.random.permutation(S)[:V]),
    }


def reference(x_words, x_scales, w1, w2_words, w2_scales, w3_words, w3_scales, offs, cen, pos1, pos2, pos3):
    xq = unpack_weight(x_words, x_scales)[:, unstriped(offs)]
    h = relu(mxq(f64(w1), 0, "e4m3").T @ xq)
    g = h[:, unstriped(cen)]
    z = np.maximum(np.maximum(h[:, unstriped(pos1)], h[:, unstriped(pos2)]), h[:, unstriped(pos3)])
    out_0 = unpack_weight(w2_words, w2_scales).T @ mxq(g, 0, "e4m3") + unpack_weight(w3_words, w3_scales).T @ mxq(z, 0, "e4m3")
    return (out_0,) + planes(out_0)

@@ -1,0 +1,185 @@
+from contextlib import ExitStack
+
+import concourse.mybir as mybir
+
+F32 = mybir.dt.float32
+BF16 = mybir.dt.bfloat16
+I32 = mybir.dt.int32
+U32 = mybir.dt.uint32
+U16 = mybir.dt.uint16
+U8 = mybir.dt.uint8
+FP8X4 = mybir.dt.float8_e4m3fn_x4
+RELU = mybir.ActivationFunctionType.Relu
+MAX = mybir.AluOpType.max
+
+P = 128
+PACK = 4
+T, S, V, H = 1024, 512, 256, 512
+HALF = V // 2
+FLOPS = 2 * 512 * H * S + 2 * 2 * H * H * V
+
+
+def words_of(dram):
+    return dram[0].rearrange("p n t -> p (n t)").bitcast(I32)
+
+
+def interleave(copy, dst, src):
+    copy(out=dst.rearrange("p (c i t) -> p c t i", i=4, t=PACK), in_=src.rearrange("p t (c i) -> p c t i", i=4))
+
+
+def tile_picked_sagecat_max_po_kernel(
+    tc, x_words, x_scales, w1, w2_words, w2_scales, w3_words, w3_scales, offs, cen, pos1, pos2, pos3, out_0, out_1, out_2
+):
+    nc = tc.nc
+    with ExitStack() as ctx:
+        lists = ctx.enter_context(tc.tile_pool(name="lists", bufs=1))
+        sb = ctx.enter_context(tc.tile_pool(name="sb", bufs=1))
+        psum = ctx.enter_context(tc.psum_pool(name="psum", bufs=1))
+
+        def tile(shape, dtype, name):
+            return sb.tile(shape, dtype, name=name, align_bytes=64)
+
+        offs_t = lists.tile([P, S // 16], U16, name="offs_t")
+        cen_t = lists.tile([P, V // 16], U16, name="cen_t")
+        pos_t = [lists.tile([P, V // 16], U16, name=f"pos_t{d}") for d in range(3)]
+
+        xw = tile([P, T], I32, "xw")
+        xs = tile([P, T], U8, "xs")
+        ws = tile([P, H], U8, "ws")
+        w1_raw = [tile([P, PACK, H // 2], F32, f"w1_raw{c}") for c in range(2)]
+        w2_raw = tile([P, H], I32, "w2_raw")
+        w3_raw = tile([P, H], I32, "w3_raw")
+
+        nc.gpsimd.memset(xs[:].bitcast(I32), 0)
+        nc.vector.memset(ws[:].bitcast(I32), 0)
+
+        nc.sync.dma_start(offs_t[:], offs)
+        for q in range(4):
+            nc.scalar.dma_start(xs[32 * q : 32 * q + 4, :].bitcast(I32), x_scales[0, 4 * q : 4 * q + 4, :].bitcast(I32))
+        w1_rows = w1.rearrange("(p j) c -> p j c", j=PACK)
+        for c in range(2):
+            nc.sync.dma_start(w1_raw[c][:], w1_rows[:, :, c * (H // 2) : (c + 1) * (H // 2)])
+        nc.sync.dma_start(xw[:], words_of(x_words))
+        nc.sync.dma_start(w3_raw[:], words_of(w3_words))
+        nc.sync.dma_start(w2_raw[:], words_of(w2_words))
+        for q in range(4):
+            nc.sync.dma_start(ws[32 * q : 32 * q + 4, :].bitcast(I32), w2_scales[0, 4 * q : 4 * q + 4, :].bitcast(I32))
+            nc.gpsimd.dma_start(ws[32 * q + 4 : 32 * q + 8, :].bitcast(I32), w3_scales[0, 4 * q : 4 * q + 4, :].bitcast(I32))
+        for list_tile, dram in zip(pos_t + [cen_t], (pos1, pos2, pos3, cen)):
+            nc.sync.dma_start(list_tile[:], dram)
+
+        warm_in = tile([P, 1], F32, "warm_in")
+        warm_out = tile([P, 1], F32, "warm_out")
+        nc.gpsimd.memset(warm_in[:], 0.0)
+        nc.scalar.activation(warm_out[:], warm_in[:], RELU)
+
+        xg_s = tile([P, S], U8, "xg_s")
+        xg_w = tile([P, S], I32, "xg_w")
+        nc.vector.tensor_copy(xg_s[:], xs[:].indirect(offs_t[:]))
+
+        w1_bf = [tile([P, 2 * P * PACK], BF16, f"w1_bf{u}") for u in range(2)]
+        for c in range(2):
+            for u, copy in enumerate((nc.vector.tensor_copy, nc.scalar.copy)):
+                copy(
+                    out=w1_bf[u][:].rearrange("p (t m j) -> p m j t", t=2, j=PACK)[:, 64 * c : 64 * c + 64],
+                    in_=w1_raw[c][:].rearrange("p j (m t) -> p m j t", t=PACK)[:, :, :, 2 * u : 2 * u + 2],
+                )
+        w1_q = tile([P, H], U32, "w1_q")
+        w1_s = tile([P, H], U8, "w1_s")
+        h = [tile([P, S], F32, f"h{t}") for t in range(PACK)]
+        for t in range(2):
+            cols = slice(t * P, (t + 1) * P)
+            nc.vector.quantize_mx(
+                out=w1_q[:, cols].bitcast(FP8X4), scales=w1_s[:, cols], in_=w1_bf[0][:, t * 512 : (t + 1) * 512]
+            )
+        nc.vector.quantize_mx(out=w1_q[:, 2 * P :].bitcast(FP8X4), scales=w1_s[:, 2 * P :], in_=w1_bf[1][:])
+
+        def layer1(t, lo, hi, bank):
+            cols = slice(t * P, (t + 1) * P)
+            acc = psum.tile([P, hi - lo], F32, name=f"acc_h{t}_{lo}", tag=f"bank{bank}")
+            nc.tensor.matmul_mx(
+                out=acc[:], lhsT=w1_q[:, cols].bitcast(FP8X4), lhsT_scale=w1_s[:, cols],
+                rhs=xg_w[:, lo:hi].bitcast(FP8X4), rhs_scale=xg_s[:, lo:hi], start=True, stop=True,
+            )
+            nc.scalar.activation(h[t][:, lo:hi], acc[:], RELU)
+
+        for bank, (lo, hi) in enumerate(((0, 256), (256, 384), (384, 512))):
+            nc.vector.tensor_copy(xg_w[:, lo:hi].bitcast(U32), xw[:].bitcast(U32).indirect(offs_t[:, lo // 16 : hi // 16]))
+            layer1(0, lo, hi, 4 + bank)
+        for t in range(1, PACK):
+            layer1(t, 0, S, t)
+
+        ws_d = tile([P, H], U8, "ws_d")
+        w2_d = tile([P, H], I32, "w2_d")
+        w3_d = tile([P, H], I32, "w3_d")
+        for dealt, raw in ((w3_d, w3_raw), (w2_d, w2_raw), (ws_d, ws)):
+            nc.vector.tensor_copy(
+                out=dealt[:].rearrange("p (t m) -> p m t", t=PACK), in_=raw[:].rearrange("p (m t) -> p m t", t=PACK)
+            )
+
+        nb = [tile([P, PACK, V], BF16, f"nb{d}") for d in range(3)]
+        for t in range(PACK):
+            for d in range(3):
+                nc.vector.tensor_copy(nb[d][:, t, :], h[t][:].indirect(pos_t[d][:]))
+        max01 = tile([P, PACK, V], BF16, "max01")
+        z = tile([P, PACK, V], BF16, "z")
+        halves = [slice(a * HALF, (a + 1) * HALF) for a in range(2)]
+        for cols in halves:
+            nc.vector.tensor_tensor(max01[:, :, cols], nb[0][:, :, cols], nb[1][:, :, cols], MAX)
+        for cols in halves:
+            nc.vector.tensor_tensor(z[:, :, cols], max01[:, :, cols], nb[2][:, :, cols], MAX)
+        zi = [tile([P, HALF * PACK], BF16, f"zi{a}") for a in range(2)]
+        z_q = tile([P, V], U32, "z_q")
+        z_s = tile([P, V], U8, "z_s")
+        g_q = tile([P, V], U32, "g_q")
+        g_s = tile([P, V], U8, "g_s")
+        gi = [tile([P, HALF * PACK], BF16, f"gi{a}") for a in range(2)]
+
+        def quantize(codes, scales, a, src):
+            cols = slice(a * HALF, (a + 1) * HALF)
+            nc.vector.quantize_mx(out=codes[:, cols].bitcast(FP8X4), scales=scales[:, cols], in_=src)
+
+        acc = [[psum.tile([P, HALF], F32, name=f"acc{a}{t}", tag=f"bank{4 * (1 - a) + t}") for t in range(PACK)] for a in range(2)]
+
+        def passes(a, w_d, plane, codes, scales, first):
+            cols = slice(a * HALF, (a + 1) * HALF)
+            for t in range(PACK):
+                m = slice(t * P, (t + 1) * P)
+                nc.tensor.matmul_mx(
+                    out=acc[a][t][:], lhsT=w_d[:, m].bitcast(FP8X4), lhsT_scale=ws_d[plane:P, m],
+                    rhs=codes[:, cols].bitcast(FP8X4), rhs_scale=scales[:, cols], start=first, stop=not first,
+                )
+
+        g = [max01[:, :, halves[0]], z[:, :, halves[1]]]
+        for a in range(2):
+            interleave(nc.scalar.copy, zi[a][:], z[:, :, halves[a]])
+        for t in range(PACK):
+            nc.vector.tensor_copy(g[0][:, t, :], h[t][:].indirect(cen_t[:, 0:8]))
+        interleave(nc.scalar.copy, gi[0][:], g[0])
+        for a in range(2):
+            quantize(z_q, z_s, a, zi[a][:])
+            passes(a, w3_d, 4, z_q, z_s, True)
+        for t in range(PACK):
+            nc.vector.tensor_copy(g[1][:, t, :], h[t][:].indirect(cen_t[:, 8:16]))
+        quantize(g_q, g_s, 0, gi[0][:])
+        passes(0, w2_d, 0, g_q, g_s, False)
+        interleave(nc.vector.tensor_copy, gi[1][:], g[1])
+        quantize(g_q, g_s, 1, gi[1][:])
+        passes(1, w2_d, 0, g_q, g_s, False)
+
+        o_q = tile([P, V], I32, "o_q")
+        o_s = tile([P, V], U8, "o_s")
+        out_rows = out_0.rearrange("(p t) v -> p t v", t=PACK)
+        for a in range(2):
+            cols = slice(a * HALF, (a + 1) * HALF)
+            y = tile([P, PACK, HALF], F32, f"y{a}")
+            yi = tile([P, HALF * PACK], BF16, f"yi{a}")
+            for t in range(PACK):
+                nc.scalar.copy(y[:, t, :], acc[a][t][:])
+            nc.sync.dma_start(out_rows[:, :, cols], y[:])
+            interleave(nc.vector.tensor_copy, yi[:], y[:])
+            quantize(o_q, o_s, a, yi[:])
+            nc.sync.dma_start(words_of(out_1)[:, cols], o_q[:, cols])
+        for q in range(4):
+            queue = nc.scalar if q % 2 else nc.sync
+            queue.dma_start(out_2[0, 4 * q : 4 * q + 4, :].bitcast(I32), o_s[32 * q : 32 * q + 4, :].bitcast(I32))

@@ -36,8 +36,8 @@ def tile_picked_sagecat_max_po_kernel(
         sb = ctx.enter_context(tc.tile_pool(name="sb", bufs=1))
         psum = ctx.enter_context(tc.psum_pool(name="psum", bufs=1))
 
-        def tile(shape, dtype, name):
-            return sb.tile(shape, dtype, name=name, align_bytes=64)
+        def tile(shape, dtype, name, tag=None):
+            return sb.tile(shape, dtype, name=name, tag=tag or name, align_bytes=64)
 
         offs_t = lists.tile([P, S // 16], U16, name="offs_t")
         cen_t = lists.tile([P, V // 16], U16, name="cen_t")
@@ -54,11 +54,11 @@ def tile_picked_sagecat_max_po_kernel(
         nc.vector.memset(ws[:].bitcast(I32), 0)
 
         nc.sync.dma_start(offs_t[:], offs)
-        for q in range(4):
-            nc.scalar.dma_start(xs[32 * q : 32 * q + 4, :].bitcast(I32), x_scales[0, 4 * q : 4 * q + 4, :].bitcast(I32))
         w1_rows = w1.rearrange("(p j) c -> p j c", j=PACK)
-        for c in range(2):
-            nc.sync.dma_start(w1_raw[c][:], w1_rows[:, :, c * (H // 2) : (c + 1) * (H // 2)])
+        nc.sync.dma_start(w1_raw[0][:], w1_rows[:, :, 0 : H // 2])
+        for q in range(4):
+            nc.sync.dma_start(xs[32 * q : 32 * q + 4, :].bitcast(I32), x_scales[0, 4 * q : 4 * q + 4, :].bitcast(I32))
+        nc.sync.dma_start(w1_raw[1][:], w1_rows[:, :, H // 2 : H])
         nc.sync.dma_start(xw[:], words_of(x_words))
         nc.sync.dma_start(w3_raw[:], words_of(w3_words))
         nc.sync.dma_start(w2_raw[:], words_of(w2_words))
@@ -79,7 +79,7 @@ def tile_picked_sagecat_max_po_kernel(
 
         w1_bf = [tile([P, 2 * P * PACK], BF16, f"w1_bf{u}") for u in range(2)]
         for c in range(2):
-            for u, copy in enumerate((nc.vector.tensor_copy, nc.scalar.copy)):
+            for u, copy in enumerate((nc.vector.tensor_copy if c else nc.scalar.copy, nc.scalar.copy)):
                 copy(
                     out=w1_bf[u][:].rearrange("p (t m j) -> p m j t", t=2, j=PACK)[:, 64 * c : 64 * c + 64],
                     in_=w1_raw[c][:].rearrange("p j (m t) -> p m j t", t=PACK)[:, :, :, 2 * u : 2 * u + 2],
@@ -92,7 +92,6 @@ def tile_picked_sagecat_max_po_kernel(
             nc.vector.quantize_mx(
                 out=w1_q[:, cols].bitcast(FP8X4), scales=w1_s[:, cols], in_=w1_bf[0][:, t * 512 : (t + 1) * 512]
             )
-        nc.vector.quantize_mx(out=w1_q[:, 2 * P :].bitcast(FP8X4), scales=w1_s[:, 2 * P :], in_=w1_bf[1][:])
 
         def layer1(t, lo, hi, bank):
             cols = slice(t * P, (t + 1) * P)
@@ -106,10 +105,11 @@ def tile_picked_sagecat_max_po_kernel(
         for bank, (lo, hi) in enumerate(((0, 256), (256, 384), (384, 512))):
             nc.vector.tensor_copy(xg_w[:, lo:hi].bitcast(U32), xw[:].bitcast(U32).indirect(offs_t[:, lo // 16 : hi // 16]))
             layer1(0, lo, hi, 4 + bank)
+        nc.vector.quantize_mx(out=w1_q[:, 2 * P :].bitcast(FP8X4), scales=w1_s[:, 2 * P :], in_=w1_bf[1][:])
         for t in range(1, PACK):
             layer1(t, 0, S, t)
 
-        ws_d = tile([P, H], U8, "ws_d")
+        ws_d = tile([P, H], U8, "ws_d", tag="w1_s")
         w2_d = tile([P, H], I32, "w2_d")
         w3_d = tile([P, H], I32, "w3_d")
         for dealt, raw in ((w3_d, w3_raw), (w2_d, w2_raw), (ws_d, ws)):
@@ -122,7 +122,7 @@ def tile_picked_sagecat_max_po_kernel(
             for d in range(3):
                 nc.vector.tensor_copy(nb[d][:, t, :], h[t][:].indirect(pos_t[d][:]))
         max01 = tile([P, PACK, V], BF16, "max01")
-        z = tile([P, PACK, V], BF16, "z")
+        z = tile([P, PACK, V], BF16, "z", tag="ws")
         halves = [slice(a * HALF, (a + 1) * HALF) for a in range(2)]
         for cols in halves:
             nc.vector.tensor_tensor(max01[:, :, cols], nb[0][:, :, cols], nb[1][:, :, cols], MAX)

@@ -55,11 +55,11 @@ def tile_picked_sagecat_max_po_kernel(
 
         nc.sync.dma_start(offs_t[:], offs)
         w1_rows = w1.rearrange("(p j) c -> p j c", j=PACK)
-        nc.sync.dma_start(w1_raw[0][:], w1_rows[:, :, 0 : H // 2])
+        nc.sync.dma_start(xw[:], words_of(x_words))
         for q in range(4):
             nc.sync.dma_start(xs[32 * q : 32 * q + 4, :].bitcast(I32), x_scales[0, 4 * q : 4 * q + 4, :].bitcast(I32))
-        nc.sync.dma_start(w1_raw[1][:], w1_rows[:, :, H // 2 : H])
-        nc.sync.dma_start(xw[:], words_of(x_words))
+        for c in range(2):
+            nc.sync.dma_start(w1_raw[c][:], w1_rows[:, :, c * (H // 2) : (c + 1) * (H // 2)])
         nc.sync.dma_start(w3_raw[:], words_of(w3_words))
         nc.sync.dma_start(w2_raw[:], words_of(w2_words))
         for q in range(4):
@@ -75,22 +75,28 @@ def tile_picked_sagecat_max_po_kernel(
 
         xg_s = tile([P, S], U8, "xg_s")
         xg_w = tile([P, S], I32, "xg_w")
+        nc.vector.tensor_copy(xg_w[:].bitcast(U32), xw[:].bitcast(U32).indirect(offs_t[:]))
         nc.vector.tensor_copy(xg_s[:], xs[:].indirect(offs_t[:]))
 
-        w1_bf = [tile([P, 2 * P * PACK], BF16, f"w1_bf{u}") for u in range(2)]
-        for c in range(2):
-            for u, copy in enumerate((nc.vector.tensor_copy if c else nc.scalar.copy, nc.scalar.copy)):
-                copy(
-                    out=w1_bf[u][:].rearrange("p (t m j) -> p m j t", t=2, j=PACK)[:, 64 * c : 64 * c + 64],
-                    in_=w1_raw[c][:].rearrange("p j (m t) -> p m j t", t=PACK)[:, :, :, 2 * u : 2 * u + 2],
-                )
+        w1_bf = tile([P, PACK * P * PACK], BF16, "w1_bf")
+
+        def round_w1(copy, c, t0, t1):
+            copy(
+                out=w1_bf[:].rearrange("p (t m j) -> p m j t", t=PACK, j=PACK)[:, 64 * c : 64 * c + 64, :, t0:t1],
+                in_=w1_raw[c][:].rearrange("p j (m t) -> p m j t", t=PACK)[:, :, :, t0:t1],
+            )
+
+        round_w1(nc.scalar.copy, 0, 0, 4)
+        round_w1(nc.vector.tensor_copy, 1, 0, 1)
+        round_w1(nc.vector.tensor_copy, 1, 1, 2)
+        round_w1(nc.scalar.copy, 1, 2, 4)
         w1_q = tile([P, H], U32, "w1_q")
         w1_s = tile([P, H], U8, "w1_s")
         h = [tile([P, S], F32, f"h{t}") for t in range(PACK)]
-        for t in range(2):
-            cols = slice(t * P, (t + 1) * P)
+        for t0, t1 in ((0, 1), (1, 2), (2, 4)):
+            cols = slice(t0 * P, t1 * P)
             nc.vector.quantize_mx(
-                out=w1_q[:, cols].bitcast(FP8X4), scales=w1_s[:, cols], in_=w1_bf[0][:, t * 512 : (t + 1) * 512]
+                out=w1_q[:, cols].bitcast(FP8X4), scales=w1_s[:, cols], in_=w1_bf[:, t0 * P * PACK : t1 * P * PACK]
             )
 
         def layer1(t, lo, hi, bank):
@@ -102,14 +108,12 @@ def tile_picked_sagecat_max_po_kernel(
             )
             nc.scalar.activation(h[t][:, lo:hi], acc[:], RELU)
 
-        for bank, (lo, hi) in enumerate(((0, 256), (256, 384), (384, 512))):
-            nc.vector.tensor_copy(xg_w[:, lo:hi].bitcast(U32), xw[:].bitcast(U32).indirect(offs_t[:, lo // 16 : hi // 16]))
-            layer1(0, lo, hi, 4 + bank)
-        nc.vector.quantize_mx(out=w1_q[:, 2 * P :].bitcast(FP8X4), scales=w1_s[:, 2 * P :], in_=w1_bf[1][:])
+        for piece in range(4):
+            layer1(0, piece * P, (piece + 1) * P, 4 + piece)
         for t in range(1, PACK):
             layer1(t, 0, S, t)
 
-        ws_d = tile([P, H], U8, "ws_d", tag="w1_s")
+        ws_d = tile([P, H], U8, "ws_d", tag="w1_bf")
         w2_d = tile([P, H], I32, "w2_d")
         w3_d = tile([P, H], I32, "w3_d")
         for dealt, raw in ((w3_d, w3_raw), (w2_d, w2_raw), (ws_d, ws)):

@@ -116,9 +116,13 @@ def tile_picked_sagecat_max_po_kernel(
         ws_d = tile([P, H], U8, "ws_d", tag="w1_bf")
         w2_d = tile([P, H], I32, "w2_d")
         w3_d = tile([P, H], I32, "w3_d")
-        for dealt, raw in ((w3_d, w3_raw), (w2_d, w2_raw), (ws_d, ws)):
-            nc.vector.tensor_copy(
-                out=dealt[:].rearrange("p (t m) -> p m t", t=PACK), in_=raw[:].rearrange("p (m t) -> p m t", t=PACK)
+        nc.vector.tensor_copy(
+            out=ws_d[:].rearrange("p (t m) -> p m t", t=PACK), in_=ws[:].rearrange("p (m t) -> p m t", t=PACK)
+        )
+        for dealt, raw in ((w3_d, w3_raw), (w2_d, w2_raw)):
+            nc.scalar.copy(
+                out=dealt[:].bitcast(U32).rearrange("p (t m) -> p m t", t=PACK),
+                in_=raw[:].bitcast(U32).rearrange("p (m t) -> p m t", t=PACK),
             )
 
         nb = [tile([P, PACK, V], BF16, f"nb{d}") for d in range(3)]

@@ -46,7 +46,7 @@ def tile_picked_sagecat_max_po_kernel(
         xw = tile([P, T], I32, "xw")
         xs = tile([P, T], U8, "xs")
         ws = tile([P, H], U8, "ws")
-        w1_raw = [tile([P, PACK, H // 2], F32, f"w1_raw{c}") for c in range(2)]
+        w1_raw = [tile([P, 2, H], F32, f"w1_raw{c}") for c in range(2)]
         w2_raw = tile([P, H], I32, "w2_raw")
         w3_raw = tile([P, H], I32, "w3_raw")
 
@@ -59,7 +59,7 @@ def tile_picked_sagecat_max_po_kernel(
         for q in range(4):
             nc.sync.dma_start(xs[32 * q : 32 * q + 4, :].bitcast(I32), x_scales[0, 4 * q : 4 * q + 4, :].bitcast(I32))
         for c in range(2):
-            nc.sync.dma_start(w1_raw[c][:], w1_rows[:, :, c * (H // 2) : (c + 1) * (H // 2)])
+            nc.sync.dma_start(w1_raw[c][:], w1_rows[:, 2 * c : 2 * c + 2, :])
         nc.sync.dma_start(w3_raw[:], words_of(w3_words))
         nc.sync.dma_start(w2_raw[:], words_of(w2_words))
         for q in range(4):
@@ -80,24 +80,31 @@ def tile_picked_sagecat_max_po_kernel(
 
         w1_bf = tile([P, PACK * P * PACK], BF16, "w1_bf")
 
-        def round_w1(copy, c, t0, t1):
+        def round_w1(copy, c, t0, t1, m0=0, m1=P):
             copy(
-                out=w1_bf[:].rearrange("p (t m j) -> p m j t", t=PACK, j=PACK)[:, 64 * c : 64 * c + 64, :, t0:t1],
-                in_=w1_raw[c][:].rearrange("p j (m t) -> p m j t", t=PACK)[:, :, :, t0:t1],
+                out=w1_bf[:].rearrange("p (t m j) -> p m j t", t=PACK, j=PACK)[:, m0:m1, 2 * c : 2 * c + 2, t0:t1],
+                in_=w1_raw[c][:].rearrange("p j (m t) -> p m j t", t=PACK)[:, m0:m1, :, t0:t1],
             )
 
-        round_w1(nc.scalar.copy, 0, 0, 4)
+        round_w1(nc.scalar.copy, 0, 0, 2)
+        round_w1(nc.scalar.copy, 0, 2, 4)
         round_w1(nc.vector.tensor_copy, 1, 0, 1)
-        round_w1(nc.vector.tensor_copy, 1, 1, 2)
         round_w1(nc.scalar.copy, 1, 2, 4)
         w1_q = tile([P, H], U32, "w1_q")
         w1_s = tile([P, H], U8, "w1_s")
         h = [tile([P, S], F32, f"h{t}") for t in range(PACK)]
-        for t0, t1 in ((0, 1), (1, 2), (2, 4)):
+
+        def quantize_w1(t0, t1):
             cols = slice(t0 * P, t1 * P)
             nc.vector.quantize_mx(
                 out=w1_q[:, cols].bitcast(FP8X4), scales=w1_s[:, cols], in_=w1_bf[:, t0 * P * PACK : t1 * P * PACK]
             )
+
+        quantize_w1(0, 1)
+        round_w1(nc.vector.tensor_copy, 1, 1, 2, 0, 32)
+        round_w1(nc.vector.tensor_copy, 1, 1, 2, 32, P)
+        quantize_w1(1, 2)
+        quantize_w1(2, 4)
 
         def layer1(t, lo, hi, bank):
             cols = slice(t * P, (t + 1) * P)
@@ -143,9 +150,14 @@ def tile_picked_sagecat_max_po_kernel(
         g_s = tile([P, V], U8, "g_s")
         gi = [tile([P, HALF * PACK], BF16, f"gi{a}") for a in range(2)]
 
-        def quantize(codes, scales, a, src):
-            cols = slice(a * HALF, (a + 1) * HALF)
+        def quantize(codes, scales, cols, src):
             nc.vector.quantize_mx(out=codes[:, cols].bitcast(FP8X4), scales=scales[:, cols], in_=src)
+
+        def interleave_pair(copy, staged, src, u):
+            copy(
+                out=staged.rearrange("p (c i t) -> p c t i", i=4, t=PACK)[:, :, 2 * u : 2 * u + 2, :],
+                in_=src.rearrange("p t (c i) -> p c t i", i=4)[:, :, 2 * u : 2 * u + 2, :],
+            )
 
         acc = [[psum.tile([P, HALF], F32, name=f"acc{a}{t}", tag=f"bank{4 * (1 - a) + t}") for t in range(PACK)] for a in range(2)]
 
@@ -165,28 +177,32 @@ def tile_picked_sagecat_max_po_kernel(
             nc.vector.tensor_copy(g[0][:, t, :], h[t][:].indirect(cen_t[:, 0:8]))
         interleave(nc.scalar.copy, gi[0][:], g[0])
         for a in range(2):
-            quantize(z_q, z_s, a, zi[a][:])
+            quantize(z_q, z_s, halves[a], zi[a][:])
             passes(a, w3_d, 4, z_q, z_s, True)
         for t in range(PACK):
             nc.vector.tensor_copy(g[1][:, t, :], h[t][:].indirect(cen_t[:, 8:16]))
-        quantize(g_q, g_s, 0, gi[0][:])
+        quantize(g_q, g_s, halves[0], gi[0][:])
         passes(0, w2_d, 0, g_q, g_s, False)
         interleave(nc.vector.tensor_copy, gi[1][:], g[1])
-        quantize(g_q, g_s, 1, gi[1][:])
+        quantize(g_q, g_s, halves[1], gi[1][:])
         passes(1, w2_d, 0, g_q, g_s, False)
 
         o_q = tile([P, V], I32, "o_q")
         o_s = tile([P, V], U8, "o_s")
         out_rows = out_0.rearrange("(p t) v -> p t v", t=PACK)
         for a in range(2):
-            cols = slice(a * HALF, (a + 1) * HALF)
+            cols = halves[a]
             y = tile([P, PACK, HALF], F32, f"y{a}")
             yi = tile([P, HALF * PACK], BF16, f"yi{a}")
             for t in range(PACK):
                 nc.scalar.copy(y[:, t, :], acc[a][t][:])
             nc.sync.dma_start(out_rows[:, :, cols], y[:])
-            interleave(nc.vector.tensor_copy, yi[:], y[:])
-            quantize(o_q, o_s, a, yi[:])
+            if a == 0:
+                interleave(nc.vector.tensor_copy, yi[:], y[:])
+            else:
+                for u in range(2):
+                    interleave_pair(nc.vector.tensor_copy, yi[:], y[:], u)
+            quantize(o_q, o_s, cols, yi[:])
             nc.sync.dma_start(words_of(out_1)[:, cols], o_q[:, cols])
         for q in range(4):
             queue = nc.scalar if q % 2 else nc.sync

@@ -9,6 +9,7 @@ U32 = mybir.dt.uint32
 U16 = mybir.dt.uint16
 U8 = mybir.dt.uint8
 FP8X4 = mybir.dt.float8_e4m3fn_x4
+COPY = mybir.ActivationFunctionType.Copy
 RELU = mybir.ActivationFunctionType.Relu
 MAX = mybir.AluOpType.max
 
@@ -16,6 +17,7 @@ P = 128
 PACK = 4
 T, S, V, H = 1024, 512, 256, 512
 HALF = V // 2
+W1_PARTS = ((0, 64), (64, 128))
 FLOPS = 2 * 512 * H * S + 2 * 2 * H * H * V
 
 
@@ -46,7 +48,7 @@ def tile_picked_sagecat_max_po_kernel(
         xw = tile([P, T], I32, "xw")
         xs = tile([P, T], U8, "xs")
         ws = tile([P, H], U8, "ws")
-        w1_raw = [tile([P, 2, H], F32, f"w1_raw{c}") for c in range(2)]
+        w1_raw = [tile([P, PACK, PACK * (m1 - m0)], F32, f"w1_raw{m0}") for m0, m1 in W1_PARTS]
         w2_raw = tile([P, H], I32, "w2_raw")
         w3_raw = tile([P, H], I32, "w3_raw")
 
@@ -54,24 +56,24 @@ def tile_picked_sagecat_max_po_kernel(
         nc.vector.memset(ws[:].bitcast(I32), 0)
 
         nc.sync.dma_start(offs_t[:], offs)
+
+        def scale_rows(queue, dst, first, dram, q):
+            queue.dma_start(dst[32 * q + first : 32 * q + first + 4, :].bitcast(I32), dram[0, 4 * q : 4 * q + 4, :].bitcast(I32))
+
         w1_rows = w1.rearrange("(p j) c -> p j c", j=PACK)
         nc.sync.dma_start(xw[:], words_of(x_words))
         for q in range(4):
-            nc.sync.dma_start(xs[32 * q : 32 * q + 4, :].bitcast(I32), x_scales[0, 4 * q : 4 * q + 4, :].bitcast(I32))
+            scale_rows(nc.sync, xs, 0, x_scales, q)
         for c in range(2):
-            nc.sync.dma_start(w1_raw[c][:], w1_rows[:, 2 * c : 2 * c + 2, :])
+            nc.sync.dma_start(w1_raw[c][:], w1_rows[:, :, PACK * W1_PARTS[c][0] : PACK * W1_PARTS[c][1]])
+        nc.sync.dma_start(pos_t[0][:], pos1)
+        for q in range(4):
+            scale_rows(nc.sync, ws, 0, w2_scales, q)
+            scale_rows(nc.sync if q < 2 else nc.gpsimd, ws, 4, w3_scales, q)
+        for list_tile, dram in zip(pos_t[1:] + [cen_t], (pos2, pos3, cen)):
+            nc.sync.dma_start(list_tile[:], dram)
         nc.sync.dma_start(w3_raw[:], words_of(w3_words))
         nc.sync.dma_start(w2_raw[:], words_of(w2_words))
-        for q in range(4):
-            nc.sync.dma_start(ws[32 * q : 32 * q + 4, :].bitcast(I32), w2_scales[0, 4 * q : 4 * q + 4, :].bitcast(I32))
-            nc.gpsimd.dma_start(ws[32 * q + 4 : 32 * q + 8, :].bitcast(I32), w3_scales[0, 4 * q : 4 * q + 4, :].bitcast(I32))
-        for list_tile, dram in zip(pos_t + [cen_t], (pos1, pos2, pos3, cen)):
-            nc.sync.dma_start(list_tile[:], dram)
-
-        warm_in = tile([P, 1], F32, "warm_in")
-        warm_out = tile([P, 1], F32, "warm_out")
-        nc.gpsimd.memset(warm_in[:], 0.0)
-        nc.scalar.activation(warm_out[:], warm_in[:], RELU)
 
         xg_s = tile([P, S], U8, "xg_s")
         xg_w = tile([P, S], I32, "xg_w")
@@ -80,16 +82,17 @@ def tile_picked_sagecat_max_po_kernel(
 
         w1_bf = tile([P, PACK * P * PACK], BF16, "w1_bf")
 
-        def round_w1(copy, c, t0, t1, m0=0, m1=P):
+        def round_w1(copy, c, m0, m1, t0, t1):
+            first = W1_PARTS[c][0]
             copy(
-                out=w1_bf[:].rearrange("p (t m j) -> p m j t", t=PACK, j=PACK)[:, m0:m1, 2 * c : 2 * c + 2, t0:t1],
-                in_=w1_raw[c][:].rearrange("p j (m t) -> p m j t", t=PACK)[:, m0:m1, :, t0:t1],
+                out=w1_bf[:].rearrange("p (t m j) -> p m j t", t=PACK, j=PACK)[:, m0:m1, :, t0:t1],
+                in_=w1_raw[c][:].rearrange("p j (m t) -> p m j t", t=PACK)[:, m0 - first : m1 - first, :, t0:t1],
             )
 
-        round_w1(nc.scalar.copy, 0, 0, 2)
-        round_w1(nc.scalar.copy, 0, 2, 4)
-        round_w1(nc.vector.tensor_copy, 1, 0, 1)
-        round_w1(nc.scalar.copy, 1, 2, 4)
+        round_w1(lambda out, in_: nc.scalar.activation(out, in_, COPY), 0, 0, 4, 0, 4)
+        round_w1(nc.scalar.copy, 0, 4, 64, 0, 4)
+        round_w1(nc.vector.tensor_copy, 1, 64, 128, 0, 1)
+        round_w1(nc.scalar.copy, 1, 64, 128, 1, 4)
         w1_q = tile([P, H], U32, "w1_q")
         w1_s = tile([P, H], U8, "w1_s")
         h = [tile([P, S], F32, f"h{t}") for t in range(PACK)]
@@ -101,8 +104,6 @@ def tile_picked_sagecat_max_po_kernel(
             )
 
         quantize_w1(0, 1)
-        round_w1(nc.vector.tensor_copy, 1, 1, 2, 0, 32)
-        round_w1(nc.vector.tensor_copy, 1, 1, 2, 32, P)
         quantize_w1(1, 2)
         quantize_w1(2, 4)
 
@@ -120,9 +121,9 @@ def tile_picked_sagecat_max_po_kernel(
         for t in range(1, PACK):
             layer1(t, 0, S, t)
 
-        ws_d = tile([P, H], U8, "ws_d", tag="w1_bf")
-        w2_d = tile([P, H], I32, "w2_d")
-        w3_d = tile([P, H], I32, "w3_d")
+        ws_d = tile([P, H], U8, "ws_d")
+        w2_d = tile([P, H], I32, "w2_d", tag="w1_q")
+        w3_d = tile([P, H], I32, "w3_d", tag="xg_w")
         nc.vector.tensor_copy(
             out=ws_d[:].rearrange("p (t m) -> p m t", t=PACK), in_=ws[:].rearrange("p (m t) -> p m t", t=PACK)
         )
@@ -132,18 +133,18 @@ def tile_picked_sagecat_max_po_kernel(
                 in_=raw[:].bitcast(U32).rearrange("p (m t) -> p m t", t=PACK),
             )
 
-        nb = [tile([P, PACK, V], BF16, f"nb{d}") for d in range(3)]
+        nb = [tile([P, PACK, V], BF16, f"nb{d}", tag=("ws", "nb1", "nb2")[d]) for d in range(3)]
         for t in range(PACK):
             for d in range(3):
                 nc.vector.tensor_copy(nb[d][:, t, :], h[t][:].indirect(pos_t[d][:]))
         max01 = tile([P, PACK, V], BF16, "max01")
-        z = tile([P, PACK, V], BF16, "z", tag="ws")
+        z = tile([P, PACK, V], BF16, "z")
         halves = [slice(a * HALF, (a + 1) * HALF) for a in range(2)]
         for cols in halves:
             nc.vector.tensor_tensor(max01[:, :, cols], nb[0][:, :, cols], nb[1][:, :, cols], MAX)
         for cols in halves:
             nc.vector.tensor_tensor(z[:, :, cols], max01[:, :, cols], nb[2][:, :, cols], MAX)
-        zi = [tile([P, HALF * PACK], BF16, f"zi{a}") for a in range(2)]
+        zi = [tile([P, HALF * PACK], BF16, f"zi{a}", tag=("w3_raw", "w2_raw")[a]) for a in range(2)]
         z_q = tile([P, V], U32, "z_q")
         z_s = tile([P, V], U8, "z_s")
         g_q = tile([P, V], U32, "g_q")

@@ -138,12 +138,12 @@ def tile_picked_sagecat_max_po_kernel(
             for d in range(3):
                 nc.vector.tensor_copy(nb[d][:, t, :], h[t][:].indirect(pos_t[d][:]))
         max01 = tile([P, PACK, V], BF16, "max01")
-        z = tile([P, PACK, V], BF16, "z")
+        z = tile([P, 2, PACK, HALF], BF16, "z")
         halves = [slice(a * HALF, (a + 1) * HALF) for a in range(2)]
         for cols in halves:
             nc.vector.tensor_tensor(max01[:, :, cols], nb[0][:, :, cols], nb[1][:, :, cols], MAX)
-        for cols in halves:
-            nc.vector.tensor_tensor(z[:, :, cols], max01[:, :, cols], nb[2][:, :, cols], MAX)
+        for a, cols in enumerate(halves):
+            nc.vector.tensor_tensor(z[:, a], max01[:, :, cols], nb[2][:, :, cols], MAX)
         zi = [tile([P, HALF * PACK], BF16, f"zi{a}", tag=("w3_raw", "w2_raw")[a]) for a in range(2)]
         z_q = tile([P, V], U32, "z_q")
         z_s = tile([P, V], U8, "z_s")
@@ -171,20 +171,20 @@ def tile_picked_sagecat_max_po_kernel(
                     rhs=codes[:, cols].bitcast(FP8X4), rhs_scale=scales[:, cols], start=first, stop=not first,
                 )
 
-        g = [max01[:, :, halves[0]], z[:, :, halves[1]]]
+        g = [max01[:, :, halves[0]], z[:, 1].rearrange("p t c -> p (t c)").rearrange("p (u c e) -> p u c e", u=2, e=2)]
         for a in range(2):
-            interleave(nc.scalar.copy, zi[a][:], z[:, :, halves[a]])
+            interleave(nc.scalar.copy, zi[a][:], z[:, a])
         for t in range(PACK):
             nc.vector.tensor_copy(g[0][:, t, :], h[t][:].indirect(cen_t[:, 0:8]))
         interleave(nc.scalar.copy, gi[0][:], g[0])
         for a in range(2):
             quantize(z_q, z_s, halves[a], zi[a][:])
             passes(a, w3_d, 4, z_q, z_s, True)
-        for t in range(PACK):
-            nc.vector.tensor_copy(g[1][:, t, :], h[t][:].indirect(cen_t[:, 8:16]))
+        for t in (0, 2, 1, 3):
+            nc.vector.tensor_copy(g[1][:, t // 2, :, t % 2], h[t][:].indirect(cen_t[:, 8:16]))
         quantize(g_q, g_s, halves[0], gi[0][:])
         passes(0, w2_d, 0, g_q, g_s, False)
-        interleave(nc.vector.tensor_copy, gi[1][:], g[1])
+        nc.vector.tensor_copy(gi[1][:].rearrange("p (c u e) -> p c u e", u=2, e=2), g[1].rearrange("p u c e -> p c u e"))
         quantize(g_q, g_s, halves[1], gi[1][:])
         passes(1, w2_d, 0, g_q, g_s, False)
 

@@ -55,13 +55,13 @@ def tile_picked_sagecat_max_po_kernel(
         nc.gpsimd.memset(xs[:].bitcast(I32), 0)
         nc.vector.memset(ws[:].bitcast(I32), 0)
 
-        nc.sync.dma_start(offs_t[:], offs)
 
         def scale_rows(queue, dst, first, dram, q):
             queue.dma_start(dst[32 * q + first : 32 * q + first + 4, :].bitcast(I32), dram[0, 4 * q : 4 * q + 4, :].bitcast(I32))
 
         w1_rows = w1.rearrange("(p j) c -> p j c", j=PACK)
         nc.sync.dma_start(xw[:], words_of(x_words))
+        nc.sync.dma_start(offs_t[:], offs)
         for q in range(4):
             scale_rows(nc.sync, xs, 0, x_scales, q)
         for c in range(2):

@@ -206,5 +206,5 @@ def tile_picked_sagecat_max_po_kernel(
             quantize(o_q, o_s, cols, yi[:])
             nc.sync.dma_start(words_of(out_1)[:, cols], o_q[:, cols])
         for q in range(4):
-            queue = nc.scalar if q % 2 else nc.sync
+            queue = nc.scalar if q == 3 else nc.sync
             queue.dma_start(out_2[0, 4 * q : 4 * q + 4, :].bitcast(I32), o_s[32 * q : 32 * q + 4, :].bitcast(I32))

@@ -41,6 +41,15 @@ def tile_picked_sagecat_max_po_kernel(
         def tile(shape, dtype, name, tag=None):
             return sb.tile(shape, dtype, name=name, tag=tag or name, align_bytes=64)
 
+        def quantize(codes, scales, cols, src):
+            nc.vector.quantize_mx(out=codes[:, cols].bitcast(FP8X4), scales=scales[:, cols], in_=src)
+
+        def vector_gather(out, window, offsets):
+            nc.vector.tensor_copy(out, window.indirect(offsets))
+
+        def scalar_gather(out, window, offsets):
+            nc.scalar.activation(out, window.indirect(offsets), COPY)
+
         offs_t = lists.tile([P, S // 16], U16, name="offs_t")
         cen_t = lists.tile([P, V // 16], U16, name="cen_t")
         pos_t = [lists.tile([P, V // 16], U16, name=f"pos_t{d}") for d in range(3)]
@@ -55,7 +64,6 @@ def tile_picked_sagecat_max_po_kernel(
         nc.gpsimd.memset(xs[:].bitcast(I32), 0)
         nc.vector.memset(ws[:].bitcast(I32), 0)
 
-
         def scale_rows(queue, dst, first, dram, q):
             queue.dma_start(dst[32 * q + first : 32 * q + first + 4, :].bitcast(I32), dram[0, 4 * q : 4 * q + 4, :].bitcast(I32))
 
@@ -66,19 +74,19 @@ def tile_picked_sagecat_max_po_kernel(
             scale_rows(nc.sync, xs, 0, x_scales, q)
         for c in range(2):
             nc.sync.dma_start(w1_raw[c][:], w1_rows[:, :, PACK * W1_PARTS[c][0] : PACK * W1_PARTS[c][1]])
-        nc.sync.dma_start(pos_t[0][:], pos1)
-        for q in range(4):
-            scale_rows(nc.sync, ws, 0, w2_scales, q)
-            scale_rows(nc.sync if q < 2 else nc.gpsimd, ws, 4, w3_scales, q)
-        for list_tile, dram in zip(pos_t[1:] + [cen_t], (pos2, pos3, cen)):
+        for list_tile, dram in zip(pos_t[:2] + [cen_t], (pos1, pos2, cen)):
             nc.sync.dma_start(list_tile[:], dram)
-        nc.sync.dma_start(w3_raw[:], words_of(w3_words))
         nc.sync.dma_start(w2_raw[:], words_of(w2_words))
+        nc.sync.dma_start(w3_raw[:], words_of(w3_words))
+        for q in range(4):
+            scale_rows(nc.sync, ws, 4, w3_scales, q)
+            scale_rows(nc.sync, ws, 0, w2_scales, q)
+        nc.sync.dma_start(pos_t[2][:], pos3)
 
         xg_s = tile([P, S], U8, "xg_s")
         xg_w = tile([P, S], I32, "xg_w")
-        nc.vector.tensor_copy(xg_w[:].bitcast(U32), xw[:].bitcast(U32).indirect(offs_t[:]))
-        nc.vector.tensor_copy(xg_s[:], xs[:].indirect(offs_t[:]))
+        vector_gather(xg_w[:].bitcast(U32), xw[:].bitcast(U32), offs_t[:])
+        vector_gather(xg_s[:], xs[:], offs_t[:])
 
         w1_bf = tile([P, PACK * P * PACK], BF16, "w1_bf")
 
@@ -97,15 +105,8 @@ def tile_picked_sagecat_max_po_kernel(
         w1_s = tile([P, H], U8, "w1_s")
         h = [tile([P, S], F32, f"h{t}") for t in range(PACK)]
 
-        def quantize_w1(t0, t1):
-            cols = slice(t0 * P, t1 * P)
-            nc.vector.quantize_mx(
-                out=w1_q[:, cols].bitcast(FP8X4), scales=w1_s[:, cols], in_=w1_bf[:, t0 * P * PACK : t1 * P * PACK]
-            )
-
-        quantize_w1(0, 1)
-        quantize_w1(1, 2)
-        quantize_w1(2, 4)
+        for t0, t1 in ((0, 1), (1, 2), (2, 4)):
+            quantize(w1_q, w1_s, slice(t0 * P, t1 * P), w1_bf[:, t0 * P * PACK : t1 * P * PACK])
 
         def layer1(t, lo, hi, bank):
             cols = slice(t * P, (t + 1) * P)
@@ -122,71 +123,54 @@ def tile_picked_sagecat_max_po_kernel(
             layer1(t, 0, S, t)
 
         ws_d = tile([P, H], U8, "ws_d")
-        w2_d = tile([P, H], I32, "w2_d", tag="w1_q")
-        w3_d = tile([P, H], I32, "w3_d", tag="xg_w")
-        nc.vector.tensor_copy(
-            out=ws_d[:].rearrange("p (t m) -> p m t", t=PACK), in_=ws[:].rearrange("p (m t) -> p m t", t=PACK)
-        )
-        for dealt, raw in ((w3_d, w3_raw), (w2_d, w2_raw)):
-            nc.scalar.copy(
-                out=dealt[:].bitcast(U32).rearrange("p (t m) -> p m t", t=PACK),
-                in_=raw[:].bitcast(U32).rearrange("p (m t) -> p m t", t=PACK),
+        w_dealt = tile([P, 2, H], I32, "w_dealt", tag="w1_bf")
+        w2_d, w3_d = w_dealt[:, 0, :], w_dealt[:, 1, :]
+        for dealt, raw in ((w2_d, w2_raw), (w3_d, w3_raw), (ws_d[:], ws)):
+            nc.vector.tensor_copy(
+                out=dealt.rearrange("p (t m) -> p m t", t=PACK), in_=raw[:].rearrange("p (m t) -> p m t", t=PACK)
             )
 
-        nb = [tile([P, PACK, V], BF16, f"nb{d}", tag=("ws", "nb1", "nb2")[d]) for d in range(3)]
-        for t in range(PACK):
-            for d in range(3):
-                nc.vector.tensor_copy(nb[d][:, t, :], h[t][:].indirect(pos_t[d][:]))
-        max01 = tile([P, PACK, V], BF16, "max01")
-        z = tile([P, 2, PACK, HALF], BF16, "z")
         halves = [slice(a * HALF, (a + 1) * HALF) for a in range(2)]
-        for cols in halves:
-            nc.vector.tensor_tensor(max01[:, :, cols], nb[0][:, :, cols], nb[1][:, :, cols], MAX)
-        for a, cols in enumerate(halves):
-            nc.vector.tensor_tensor(z[:, a], max01[:, :, cols], nb[2][:, :, cols], MAX)
-        zi = [tile([P, HALF * PACK], BF16, f"zi{a}", tag=("w3_raw", "w2_raw")[a]) for a in range(2)]
+        g = tile([P, PACK, V], BF16, "g")
+        nb = [tile([P, PACK, V], BF16, f"nb{d}") for d in range(2)]
+        for t in range(PACK):
+            scalar_gather(g[:, t, :], h[t][:], cen_t[:])
+        for t in range(PACK):
+            vector_gather(nb[0][:, t, :], h[t][:], pos_t[0][:])
+            (vector_gather if t < 3 else scalar_gather)(nb[1][:, t, :], h[t][:], pos_t[1][:])
+        last = [tile([P, PACK, HALF], BF16, f"last{a}") for a in range(2)]
+        for a in range(2):
+            for t in range(PACK):
+                scalar_gather(last[a][:, t, :], h[t][:], pos_t[2][:, 8 * a : 8 * a + 8])
+
         z_q = tile([P, V], U32, "z_q")
         z_s = tile([P, V], U8, "z_s")
         g_q = tile([P, V], U32, "g_q")
         g_s = tile([P, V], U8, "g_s")
-        gi = [tile([P, HALF * PACK], BF16, f"gi{a}") for a in range(2)]
-
-        def quantize(codes, scales, cols, src):
-            nc.vector.quantize_mx(out=codes[:, cols].bitcast(FP8X4), scales=scales[:, cols], in_=src)
-
-        def interleave_pair(copy, staged, src, u):
-            copy(
-                out=staged.rearrange("p (c i t) -> p c t i", i=4, t=PACK)[:, :, 2 * u : 2 * u + 2, :],
-                in_=src.rearrange("p t (c i) -> p c t i", i=4)[:, :, 2 * u : 2 * u + 2, :],
-            )
-
         acc = [[psum.tile([P, HALF], F32, name=f"acc{a}{t}", tag=f"bank{4 * (1 - a) + t}") for t in range(PACK)] for a in range(2)]
 
         def passes(a, w_d, plane, codes, scales, first):
-            cols = slice(a * HALF, (a + 1) * HALF)
             for t in range(PACK):
                 m = slice(t * P, (t + 1) * P)
                 nc.tensor.matmul_mx(
                     out=acc[a][t][:], lhsT=w_d[:, m].bitcast(FP8X4), lhsT_scale=ws_d[plane:P, m],
-                    rhs=codes[:, cols].bitcast(FP8X4), rhs_scale=scales[:, cols], start=first, stop=not first,
+                    rhs=codes[:, halves[a]].bitcast(FP8X4), rhs_scale=scales[:, halves[a]], start=first, stop=not first,
                 )
 
-        g = [max01[:, :, halves[0]], z[:, 1].rearrange("p t c -> p (t c)").rearrange("p (u c e) -> p u c e", u=2, e=2)]
+        gi = tile([P, V * PACK], BF16, "gi")
+        interleave(nc.vector.tensor_copy, gi[:], g[:])
+        max01 = tile([P, PACK, V], BF16, "max01")
+        nc.vector.tensor_tensor(max01[:], nb[0][:], nb[1][:], MAX)
+        quantize(g_q, g_s, slice(0, V), gi[:])
         for a in range(2):
-            interleave(nc.scalar.copy, zi[a][:], z[:, a])
-        for t in range(PACK):
-            nc.vector.tensor_copy(g[0][:, t, :], h[t][:].indirect(cen_t[:, 0:8]))
-        interleave(nc.scalar.copy, gi[0][:], g[0])
+            passes(a, w2_d, 0, g_q, g_s, True)
         for a in range(2):
-            quantize(z_q, z_s, halves[a], zi[a][:])
-            passes(a, w3_d, 4, z_q, z_s, True)
-        for t in (0, 2, 1, 3):
-            nc.vector.tensor_copy(g[1][:, t // 2, :, t % 2], h[t][:].indirect(cen_t[:, 8:16]))
-        quantize(g_q, g_s, halves[0], gi[0][:])
-        passes(0, w2_d, 0, g_q, g_s, False)
-        nc.vector.tensor_copy(gi[1][:].rearrange("p (c u e) -> p c u e", u=2, e=2), g[1].rearrange("p u c e -> p c u e"))
-        quantize(g_q, g_s, halves[1], gi[1][:])
-        passes(1, w2_d, 0, g_q, g_s, False)
+            z = tile([P, PACK, HALF], BF16, f"z{a}")
+            zi = tile([P, HALF * PACK], BF16, f"zi{a}")
+            nc.vector.tensor_tensor(z[:], max01[:, :, halves[a]], last[a][:], MAX)
+            interleave(nc.vector.tensor_copy, zi[:], z[:])
+            quantize(z_q, z_s, halves[a], zi[:])
+            passes(a, w3_d, 4, z_q, z_s, False)
 
         o_q = tile([P, V], I32, "o_q")
         o_s = tile([P, V], U8, "o_s")
@@ -198,11 +182,12 @@ def tile_picked_sagecat_max_po_kernel(
             for t in range(PACK):
                 nc.scalar.copy(y[:, t, :], acc[a][t][:])
             nc.sync.dma_start(out_rows[:, :, cols], y[:])
-            if a == 0:
-                interleave(nc.vector.tensor_copy, yi[:], y[:])
-            else:
-                for u in range(2):
-                    interleave_pair(nc.vector.tensor_copy, yi[:], y[:], u)
+            pieces = ((0, 4),) if a == 0 else ((0, 2), (2, 4))
+            for t0, t1 in pieces:
+                nc.vector.tensor_copy(
+                    out=yi[:].rearrange("p (c i t) -> p c t i", i=4, t=PACK)[:, :, t0:t1, :],
+                    in_=y[:].rearrange("p t (c i) -> p c t i", i=4)[:, :, t0:t1, :],
+                )
             quantize(o_q, o_s, cols, yi[:])
             nc.sync.dma_start(words_of(out_1)[:, cols], o_q[:, cols])
         for q in range(4):

@@ -122,22 +122,20 @@ def tile_picked_sagecat_max_po_kernel(
         for t in range(1, PACK):
             layer1(t, 0, S, t)
 
-        ws_d = tile([P, H], U8, "ws_d")
         w_dealt = tile([P, 2, H], I32, "w_dealt", tag="w1_bf")
         w2_d, w3_d = w_dealt[:, 0, :], w_dealt[:, 1, :]
-        for dealt, raw in ((w2_d, w2_raw), (w3_d, w3_raw), (ws_d[:], ws)):
+        for dealt, raw in ((w2_d, w2_raw), (w3_d, w3_raw)):
             nc.vector.tensor_copy(
                 out=dealt.rearrange("p (t m) -> p m t", t=PACK), in_=raw[:].rearrange("p (m t) -> p m t", t=PACK)
             )
 
         halves = [slice(a * HALF, (a + 1) * HALF) for a in range(2)]
-        g = tile([P, PACK, V], BF16, "g")
+        g = tile([P, 2, V, 2], BF16, "g")
         nb = [tile([P, PACK, V], BF16, f"nb{d}") for d in range(2)]
         for t in range(PACK):
-            scalar_gather(g[:, t, :], h[t][:], cen_t[:])
-        for t in range(PACK):
+            vector_gather(g[:, t // 2, :, t % 2], h[t][:], cen_t[:])
             vector_gather(nb[0][:, t, :], h[t][:], pos_t[0][:])
-            (vector_gather if t < 3 else scalar_gather)(nb[1][:, t, :], h[t][:], pos_t[1][:])
+            scalar_gather(nb[1][:, t, :], h[t][:], pos_t[1][:])
         last = [tile([P, PACK, HALF], BF16, f"last{a}") for a in range(2)]
         for a in range(2):
             for t in range(PACK):
@@ -158,10 +156,14 @@ def tile_picked_sagecat_max_po_kernel(
                 )
 
         gi = tile([P, V * PACK], BF16, "gi")
-        interleave(nc.vector.tensor_copy, gi[:], g[:])
+        nc.vector.tensor_copy(gi[:].rearrange("p (c u e) -> p c u e", u=2, e=2), g[:].rearrange("p u c e -> p c u e"))
+        ws_d = tile([P, H], U8, "ws_d", tag="g")
+        nc.vector.tensor_copy(
+            out=ws_d[:].rearrange("p (t m) -> p m t", t=PACK), in_=ws[:].rearrange("p (m t) -> p m t", t=PACK)
+        )
         max01 = tile([P, PACK, V], BF16, "max01")
-        nc.vector.tensor_tensor(max01[:], nb[0][:], nb[1][:], MAX)
         quantize(g_q, g_s, slice(0, V), gi[:])
+        nc.vector.tensor_tensor(max01[:], nb[0][:], nb[1][:], MAX)
         for a in range(2):
             passes(a, w2_d, 0, g_q, g_s, True)
         for a in range(2):

@@ -17,7 +17,7 @@ P = 128
 PACK = 4
 T, S, V, H = 1024, 512, 256, 512
 HALF = V // 2
-W1_PARTS = ((0, 64), (64, 128))
+W1_PARTS = ((0, 44), (44, 92), (92, 128))
 FLOPS = 2 * 512 * H * S + 2 * 2 * H * H * V
 
 
@@ -68,11 +68,11 @@ def tile_picked_sagecat_max_po_kernel(
             queue.dma_start(dst[32 * q + first : 32 * q + first + 4, :].bitcast(I32), dram[0, 4 * q : 4 * q + 4, :].bitcast(I32))
 
         w1_rows = w1.rearrange("(p j) c -> p j c", j=PACK)
-        nc.sync.dma_start(xw[:], words_of(x_words))
         nc.sync.dma_start(offs_t[:], offs)
+        nc.sync.dma_start(xw[:], words_of(x_words))
         for q in range(4):
             scale_rows(nc.sync, xs, 0, x_scales, q)
-        for c in range(2):
+        for c in range(len(W1_PARTS)):
             nc.sync.dma_start(w1_raw[c][:], w1_rows[:, :, PACK * W1_PARTS[c][0] : PACK * W1_PARTS[c][1]])
         for list_tile, dram in zip(pos_t[:2] + [cen_t], (pos1, pos2, cen)):
             nc.sync.dma_start(list_tile[:], dram)
@@ -98,9 +98,11 @@ def tile_picked_sagecat_max_po_kernel(
             )
 
         round_w1(lambda out, in_: nc.scalar.activation(out, in_, COPY), 0, 0, 4, 0, 4)
-        round_w1(nc.scalar.copy, 0, 4, 64, 0, 4)
-        round_w1(nc.vector.tensor_copy, 1, 64, 128, 0, 1)
-        round_w1(nc.scalar.copy, 1, 64, 128, 1, 4)
+        round_w1(nc.scalar.copy, 0, 4, W1_PARTS[0][1], 0, 4)
+        for c in range(1, len(W1_PARTS) - 1):
+            round_w1(nc.scalar.copy, c, *W1_PARTS[c], 0, 4)
+        for t0 in (0, 2):
+            round_w1(nc.vector.tensor_copy, len(W1_PARTS) - 1, *W1_PARTS[-1], t0, t0 + 2)
         w1_q = tile([P, H], U32, "w1_q")
         w1_s = tile([P, H], U8, "w1_s")
         h = [tile([P, S], F32, f"h{t}") for t in range(PACK)]
@@ -117,29 +119,30 @@ def tile_picked_sagecat_max_po_kernel(
             )
             nc.scalar.activation(h[t][:, lo:hi], acc[:], RELU)
 
-        for piece in range(4):
-            layer1(0, piece * P, (piece + 1) * P, 4 + piece)
-        for t in range(1, PACK):
-            layer1(t, 0, S, t)
-
+        ws_d = tile([P, H], U8, "ws_d")
         w_dealt = tile([P, 2, H], I32, "w_dealt", tag="w1_bf")
         w2_d, w3_d = w_dealt[:, 0, :], w_dealt[:, 1, :]
-        for dealt, raw in ((w2_d, w2_raw), (w3_d, w3_raw)):
-            nc.vector.tensor_copy(
-                out=dealt.rearrange("p (t m) -> p m t", t=PACK), in_=raw[:].rearrange("p (m t) -> p m t", t=PACK)
+        for dealt, raw in ((w2_d, w2_raw), (ws_d[:], ws), (w3_d, w3_raw)):
+            nc.gpsimd.tensor_copy(
+                out=dealt.rearrange("p (t m) -> p t m", t=PACK), in_=raw[:].rearrange("p (m t) -> p t m", t=PACK)
             )
 
         halves = [slice(a * HALF, (a + 1) * HALF) for a in range(2)]
         g = tile([P, 2, V, 2], BF16, "g")
-        nb = [tile([P, PACK, V], BF16, f"nb{d}") for d in range(2)]
+        shared = tile([P, 3 * HALF + PACK * V], BF16, "shared")
+        nb = [shared[:, 3 * HALF :].rearrange("p (t c) -> p t c", t=PACK), tile([P, PACK, V], BF16, "nb1")]
         for t in range(PACK):
+            pieces = 4 if t == 0 else 1
+            for piece in range(pieces):
+                layer1(t, piece * S // pieces, (piece + 1) * S // pieces, 4 + piece if t == 0 else t)
             vector_gather(g[:, t // 2, :, t % 2], h[t][:], cen_t[:])
             vector_gather(nb[0][:, t, :], h[t][:], pos_t[0][:])
             scalar_gather(nb[1][:, t, :], h[t][:], pos_t[1][:])
-        last = [tile([P, PACK, HALF], BF16, f"last{a}") for a in range(2)]
-        for a in range(2):
-            for t in range(PACK):
-                scalar_gather(last[a][:, t, :], h[t][:], pos_t[2][:, 8 * a : 8 * a + 8])
+        last = [tile([P, PACK, HALF], BF16, "last0")[:], shared[:, : PACK * HALF].rearrange("p (t c) -> p t c", t=PACK)]
+        for t in range(PACK):
+            scalar_gather(last[0][:, t, :], h[t][:], pos_t[2][:, 0:8])
+        for t in range(PACK - 1):
+            scalar_gather(last[1][:, t, :], h[t][:], pos_t[2][:, 8:16])
 
         z_q = tile([P, V], U32, "z_q")
         z_s = tile([P, V], U8, "z_s")
@@ -157,20 +160,22 @@ def tile_picked_sagecat_max_po_kernel(
 
         gi = tile([P, V * PACK], BF16, "gi")
         nc.vector.tensor_copy(gi[:].rearrange("p (c u e) -> p c u e", u=2, e=2), g[:].rearrange("p u c e -> p c u e"))
-        ws_d = tile([P, H], U8, "ws_d", tag="g")
-        nc.vector.tensor_copy(
-            out=ws_d[:].rearrange("p (t m) -> p m t", t=PACK), in_=ws[:].rearrange("p (m t) -> p m t", t=PACK)
-        )
         max01 = tile([P, PACK, V], BF16, "max01")
         quantize(g_q, g_s, slice(0, V), gi[:])
-        nc.vector.tensor_tensor(max01[:], nb[0][:], nb[1][:], MAX)
+        for cols in halves:
+            nc.vector.tensor_tensor(max01[:, :, cols], nb[0][:, :, cols], nb[1][:, :, cols], MAX)
         for a in range(2):
             passes(a, w2_d, 0, g_q, g_s, True)
         for a in range(2):
-            z = tile([P, PACK, HALF], BF16, f"z{a}")
             zi = tile([P, HALF * PACK], BF16, f"zi{a}")
-            nc.vector.tensor_tensor(z[:], max01[:, :, halves[a]], last[a][:], MAX)
-            interleave(nc.vector.tensor_copy, zi[:], z[:])
+            nc.vector.tensor_tensor(
+                zi[:].rearrange("p (c i t) -> p c t i", i=4, t=PACK),
+                max01[:, :, halves[a]].rearrange("p t (c i) -> p c t i", i=4),
+                last[a].rearrange("p t (c i) -> p c t i", i=4),
+                MAX,
+            )
+            if a == 0:
+                vector_gather(last[1][:, PACK - 1, :], h[PACK - 1][:], pos_t[2][:, 8:16])
             quantize(z_q, z_s, halves[a], zi[:])
             passes(a, w3_d, 4, z_q, z_s, False)
 

@@ -36,6 +36,7 @@ def tile_picked_sagecat_max_po_kernel(
     with ExitStack() as ctx:
         lists = ctx.enter_context(tc.tile_pool(name="lists", bufs=1))
         sb = ctx.enter_context(tc.tile_pool(name="sb", bufs=1))
+        reused = ctx.enter_context(tc.tile_pool(name="reused", bufs=1))
         psum = ctx.enter_context(tc.psum_pool(name="psum", bufs=1))
 
         def tile(shape, dtype, name, tag=None):
@@ -56,7 +57,7 @@ def tile_picked_sagecat_max_po_kernel(
 
         xw = tile([P, T], I32, "xw")
         xs = tile([P, T], U8, "xs")
-        ws = tile([P, H], U8, "ws")
+        ws = reused.tile([P, H], U8, name="ws", align_bytes=64, offset=2 * PACK * V - H // 2)
         w1_raw = [tile([P, PACK, PACK * (m1 - m0)], F32, f"w1_raw{m0}") for m0, m1 in W1_PARTS]
         w2_raw = tile([P, H], I32, "w2_raw")
         w3_raw = tile([P, H], I32, "w3_raw")
@@ -129,13 +130,15 @@ def tile_picked_sagecat_max_po_kernel(
 
         halves = [slice(a * HALF, (a + 1) * HALF) for a in range(2)]
         g = tile([P, 2, V, 2], BF16, "g")
-        shared = tile([P, 3 * HALF + PACK * V], BF16, "shared")
+        shared = reused.tile([P, 3 * HALF + PACK * V], BF16, name="shared", align_bytes=64, offset=2 * PACK * V)
         nb = [shared[:, 3 * HALF :].rearrange("p (t c) -> p t c", t=PACK), tile([P, PACK, V], BF16, "nb1")]
+        for piece in range(4):
+            layer1(0, piece * P, (piece + 1) * P, 4 + piece)
+        for t in range(1, PACK):
+            layer1(t, 0, S, t)
         for t in range(PACK):
-            pieces = 4 if t == 0 else 1
-            for piece in range(pieces):
-                layer1(t, piece * S // pieces, (piece + 1) * S // pieces, 4 + piece if t == 0 else t)
             vector_gather(g[:, t // 2, :, t % 2], h[t][:], cen_t[:])
+        for t in range(PACK):
             vector_gather(nb[0][:, t, :], h[t][:], pos_t[0][:])
             scalar_gather(nb[1][:, t, :], h[t][:], pos_t[1][:])
         last = [tile([P, PACK, HALF], BF16, "last0")[:], shared[:, : PACK * HALF].rearrange("p (t c) -> p t c", t=PACK)]
@@ -158,10 +161,13 @@ def tile_picked_sagecat_max_po_kernel(
                     rhs=codes[:, halves[a]].bitcast(FP8X4), rhs_scale=scales[:, halves[a]], start=first, stop=not first,
                 )
 
-        gi = tile([P, V * PACK], BF16, "gi")
-        nc.vector.tensor_copy(gi[:].rearrange("p (c u e) -> p c u e", u=2, e=2), g[:].rearrange("p u c e -> p c u e"))
-        max01 = tile([P, PACK, V], BF16, "max01")
+        gi = reused.tile([P, V * PACK], BF16, name="gi", align_bytes=64, offset=0)
+        nc.gpsimd.tensor_copy(
+            gi[:].bitcast(I32).rearrange("p (c u) -> p c u", u=2),
+            g[:].rearrange("p u c e -> p (u c e)").bitcast(I32).rearrange("p (u c) -> p c u", u=2),
+        )
         quantize(g_q, g_s, slice(0, V), gi[:])
+        max01 = tile([P, PACK, V], BF16, "max01")
         for cols in halves:
             nc.vector.tensor_tensor(max01[:, :, cols], nb[0][:, :, cols], nb[1][:, :, cols], MAX)
         for a in range(2):

@@ -130,8 +130,7 @@ def tile_picked_sagecat_max_po_kernel(
 
         halves = [slice(a * HALF, (a + 1) * HALF) for a in range(2)]
         g = tile([P, 2, V, 2], BF16, "g")
-        shared = reused.tile([P, 3 * HALF + PACK * V], BF16, name="shared", align_bytes=64, offset=2 * PACK * V)
-        nb = [shared[:, 3 * HALF :].rearrange("p (t c) -> p t c", t=PACK), tile([P, PACK, V], BF16, "nb1")]
+        nb = [reused.tile([P, PACK, V], BF16, name="nb0", align_bytes=64, offset=2 * PACK * V), tile([P, PACK, V], BF16, "nb1")]
         for piece in range(4):
             layer1(0, piece * P, (piece + 1) * P, 4 + piece)
         for t in range(1, PACK):
@@ -141,11 +140,9 @@ def tile_picked_sagecat_max_po_kernel(
         for t in range(PACK):
             vector_gather(nb[0][:, t, :], h[t][:], pos_t[0][:])
             scalar_gather(nb[1][:, t, :], h[t][:], pos_t[1][:])
-        last = [tile([P, PACK, HALF], BF16, "last0")[:], shared[:, : PACK * HALF].rearrange("p (t c) -> p t c", t=PACK)]
+        last = [tile([P, PACK, HALF], F32, "last0")[:]]
         for t in range(PACK):
             scalar_gather(last[0][:, t, :], h[t][:], pos_t[2][:, 0:8])
-        for t in range(PACK - 1):
-            scalar_gather(last[1][:, t, :], h[t][:], pos_t[2][:, 8:16])
 
         z_q = tile([P, V], U32, "z_q")
         z_s = tile([P, V], U8, "z_s")
@@ -167,7 +164,10 @@ def tile_picked_sagecat_max_po_kernel(
             g[:].rearrange("p u c e -> p (u c e)").bitcast(I32).rearrange("p (u c) -> p c u", u=2),
         )
         quantize(g_q, g_s, slice(0, V), gi[:])
-        max01 = tile([P, PACK, V], BF16, "max01")
+        last.append(reused.tile([P, PACK, HALF], F32, name="last1", align_bytes=64, offset=0)[:])
+        for t in range(PACK - 1):
+            scalar_gather(last[1][:, t, :], h[t][:], pos_t[2][:, 8:16])
+        max01 = tile([P, PACK, V], BF16, "max01", tag="g")
         for cols in halves:
             nc.vector.tensor_tensor(max01[:, :, cols], nb[0][:, :, cols], nb[1][:, :, cols], MAX)
         for a in range(2):

@@ -12,6 +12,8 @@ FP8X4 = mybir.dt.float8_e4m3fn_x4
 COPY = mybir.ActivationFunctionType.Copy
 RELU = mybir.ActivationFunctionType.Relu
 MAX = mybir.AluOpType.max
+MULT = mybir.AluOpType.mult
+ADD = mybir.AluOpType.add
 
 P = 128
 PACK = 4
@@ -129,14 +131,14 @@ def tile_picked_sagecat_max_po_kernel(
             )
 
         halves = [slice(a * HALF, (a + 1) * HALF) for a in range(2)]
-        g = tile([P, 2, V, 2], BF16, "g")
+        g = tile([P, PACK, V], BF16, "g")
         nb = [reused.tile([P, PACK, V], BF16, name="nb0", align_bytes=64, offset=2 * PACK * V), tile([P, PACK, V], BF16, "nb1")]
         for piece in range(4):
             layer1(0, piece * P, (piece + 1) * P, 4 + piece)
         for t in range(1, PACK):
             layer1(t, 0, S, t)
         for t in range(PACK):
-            vector_gather(g[:, t // 2, :, t % 2], h[t][:], cen_t[:])
+            vector_gather(g[:, t, :], h[t][:], cen_t[:])
         for t in range(PACK):
             vector_gather(nb[0][:, t, :], h[t][:], pos_t[0][:])
             scalar_gather(nb[1][:, t, :], h[t][:], pos_t[1][:])
@@ -159,9 +161,8 @@ def tile_picked_sagecat_max_po_kernel(
                 )
 
         gi = reused.tile([P, V * PACK], BF16, name="gi", align_bytes=64, offset=0)
-        nc.gpsimd.tensor_copy(
-            gi[:].bitcast(I32).rearrange("p (c u) -> p c u", u=2),
-            g[:].rearrange("p u c e -> p (u c e)").bitcast(I32).rearrange("p (u c) -> p c u", u=2),
+        nc.gpsimd.tensor_scalar(
+            gi[:].rearrange("p (c t) -> p c t", t=PACK), g[:].rearrange("p t c -> p c t"), 1.0, 0.0, MULT, ADD
         )
         quantize(g_q, g_s, slice(0, V), gi[:])
         last.append(reused.tile([P, PACK, HALF], F32, name="last1", align_bytes=64, offset=0)[:])

@@ -140,8 +140,11 @@ def tile_picked_sagecat_max_po_kernel(
         for t in range(PACK):
             vector_gather(g[:, t, :], h[t][:], cen_t[:])
         for t in range(PACK):
-            vector_gather(nb[0][:, t, :], h[t][:], pos_t[0][:])
             scalar_gather(nb[1][:, t, :], h[t][:], pos_t[1][:])
+            if t < PACK - 1:
+                vector_gather(nb[0][:, t, :], h[t][:], pos_t[0][:])
+        vector_gather(nb[0][:, PACK - 1, halves[0]], h[PACK - 1][:], pos_t[0][:, 0:8])
+        scalar_gather(nb[0][:, PACK - 1, halves[1]], h[PACK - 1][:], pos_t[0][:, 8:16])
         last = [tile([P, PACK, HALF], F32, "last0")[:]]
         for t in range(PACK):
             scalar_gather(last[0][:, t, :], h[t][:], pos_t[2][:, 0:8])

@@ -141,13 +141,10 @@ def tile_picked_sagecat_max_po_kernel(
             vector_gather(g[:, t, :], h[t][:], cen_t[:])
         for t in range(PACK):
             scalar_gather(nb[1][:, t, :], h[t][:], pos_t[1][:])
-            if t < PACK - 1:
-                vector_gather(nb[0][:, t, :], h[t][:], pos_t[0][:])
-        vector_gather(nb[0][:, PACK - 1, halves[0]], h[PACK - 1][:], pos_t[0][:, 0:8])
-        scalar_gather(nb[0][:, PACK - 1, halves[1]], h[PACK - 1][:], pos_t[0][:, 8:16])
+            (vector_gather if t < PACK - 1 else scalar_gather)(nb[0][:, t, :], h[t][:], pos_t[0][:])
         last = [tile([P, PACK, HALF], F32, "last0")[:]]
         for t in range(PACK):
-            scalar_gather(last[0][:, t, :], h[t][:], pos_t[2][:, 0:8])
+            (scalar_gather if t < PACK - 1 else vector_gather)(last[0][:, t, :], h[t][:], pos_t[2][:, 0:8])
 
         z_q = tile([P, V], U32, "z_q")
         z_s = tile([P, V], U8, "z_s")

@@ -19,7 +19,6 @@ P = 128
 PACK = 4
 T, S, V, H = 1024, 512, 256, 512
 HALF = V // 2
-W1_PARTS = ((0, 44), (44, 92), (92, 128))
 FLOPS = 2 * 512 * H * S + 2 * 2 * H * H * V
 
 
@@ -60,7 +59,7 @@ def tile_picked_sagecat_max_po_kernel(
         xw = tile([P, T], I32, "xw")
         xs = tile([P, T], U8, "xs")
         ws = reused.tile([P, H], U8, name="ws", align_bytes=64, offset=2 * PACK * V - H // 2)
-        w1_raw = [tile([P, PACK, PACK * (m1 - m0)], F32, f"w1_raw{m0}") for m0, m1 in W1_PARTS]
+        w1_raw = [tile([P, 2, H], F32, f"w1_raw{u}") for u in range(2)]
         w2_raw = tile([P, H], I32, "w2_raw")
         w3_raw = tile([P, H], I32, "w3_raw")
 
@@ -70,13 +69,13 @@ def tile_picked_sagecat_max_po_kernel(
         def scale_rows(queue, dst, first, dram, q):
             queue.dma_start(dst[32 * q + first : 32 * q + first + 4, :].bitcast(I32), dram[0, 4 * q : 4 * q + 4, :].bitcast(I32))
 
-        w1_rows = w1.rearrange("(p j) c -> p j c", j=PACK)
-        nc.sync.dma_start(offs_t[:], offs)
+        w1_pairs = w1.rearrange("(p u e) c -> u p e c", u=2, e=2)
         nc.sync.dma_start(xw[:], words_of(x_words))
+        nc.sync.dma_start(offs_t[:], offs)
         for q in range(4):
             scale_rows(nc.sync, xs, 0, x_scales, q)
-        for c in range(len(W1_PARTS)):
-            nc.sync.dma_start(w1_raw[c][:], w1_rows[:, :, PACK * W1_PARTS[c][0] : PACK * W1_PARTS[c][1]])
+        for u in range(2):
+            nc.sync.dma_start(w1_raw[u][:], w1_pairs[u])
         for list_tile, dram in zip(pos_t[:2] + [cen_t], (pos1, pos2, cen)):
             nc.sync.dma_start(list_tile[:], dram)
         nc.sync.dma_start(w2_raw[:], words_of(w2_words))
@@ -92,26 +91,29 @@ def tile_picked_sagecat_max_po_kernel(
         vector_gather(xg_s[:], xs[:], offs_t[:])
 
         w1_bf = tile([P, PACK * P * PACK], BF16, "w1_bf")
-
-        def round_w1(copy, c, m0, m1, t0, t1):
-            first = W1_PARTS[c][0]
-            copy(
-                out=w1_bf[:].rearrange("p (t m j) -> p m j t", t=PACK, j=PACK)[:, m0:m1, :, t0:t1],
-                in_=w1_raw[c][:].rearrange("p j (m t) -> p m j t", t=PACK)[:, m0 - first : m1 - first, :, t0:t1],
-            )
-
-        round_w1(lambda out, in_: nc.scalar.activation(out, in_, COPY), 0, 0, 4, 0, 4)
-        round_w1(nc.scalar.copy, 0, 4, W1_PARTS[0][1], 0, 4)
-        for c in range(1, len(W1_PARTS) - 1):
-            round_w1(nc.scalar.copy, c, *W1_PARTS[c], 0, 4)
-        for t0 in (0, 2):
-            round_w1(nc.vector.tensor_copy, len(W1_PARTS) - 1, *W1_PARTS[-1], t0, t0 + 2)
         w1_q = tile([P, H], U32, "w1_q")
         w1_s = tile([P, H], U8, "w1_s")
-        h = [tile([P, S], F32, f"h{t}") for t in range(PACK)]
 
-        for t0, t1 in ((0, 1), (1, 2), (2, 4)):
+        def round_w1(copy, u, m0, m1, t0, t1):
+            copy(
+                out=w1_bf[:].rearrange("p (t m u e) -> p u m t e", t=PACK, u=2, e=2)[:, u, m0:m1, t0:t1, :],
+                in_=w1_raw[u][:].rearrange("p e (m t) -> p m t e", t=PACK)[:, m0:m1, t0:t1, :],
+            )
+
+        def quantize_w1(t0, t1):
             quantize(w1_q, w1_s, slice(t0 * P, t1 * P), w1_bf[:, t0 * P * PACK : t1 * P * PACK])
+
+        round_w1(lambda out, in_: nc.scalar.activation(out, in_, COPY), 0, 0, 4, 0, 2)
+        round_w1(nc.scalar.copy, 0, 4, P, 0, 2)
+        round_w1(nc.scalar.copy, 1, 0, P, 0, 1)
+        round_w1(nc.scalar.copy, 0, 0, P, 2, 4)
+        round_w1(nc.vector.tensor_copy, 1, 0, P, 1, 2)
+        for t in range(2):
+            quantize_w1(t, t + 1)
+        round_w1(nc.vector.tensor_copy, 1, 0, P, 2, 4)
+        quantize_w1(2, 4)
+
+        h = [tile([P, S], F32, f"h{t}") for t in range(PACK)]
 
         def layer1(t, lo, hi, bank):
             cols = slice(t * P, (t + 1) * P)

@@ -52,6 +52,9 @@ def tile_picked_sagecat_max_po_kernel(
         def scalar_gather(out, window, offsets):
             nc.scalar.activation(out, window.indirect(offsets), COPY)
 
+        def gpsimd_copy(out, in_):
+            nc.gpsimd.tensor_scalar(out, in_, 1.0, 0.0, MULT, ADD)
+
         offs_t = lists.tile([P, S // 16], U16, name="offs_t")
         cen_t = lists.tile([P, V // 16], U16, name="cen_t")
         pos_t = [lists.tile([P, V // 16], U16, name=f"pos_t{d}") for d in range(3)]
@@ -105,12 +108,12 @@ def tile_picked_sagecat_max_po_kernel(
 
         round_w1(lambda out, in_: nc.scalar.activation(out, in_, COPY), 0, 0, 4, 0, 2)
         round_w1(nc.scalar.copy, 0, 4, P, 0, 2)
-        round_w1(nc.scalar.copy, 1, 0, P, 0, 1)
-        round_w1(nc.scalar.copy, 0, 0, P, 2, 4)
-        round_w1(nc.vector.tensor_copy, 1, 0, P, 1, 2)
+        round_w1(gpsimd_copy, 0, 0, P, 2, 4)
+        round_w1(nc.scalar.copy, 1, 0, P // 2, 0, 2)
+        round_w1(gpsimd_copy, 1, P // 2, P, 0, 2)
+        round_w1(nc.scalar.copy, 1, 0, P, 2, 4)
         for t in range(2):
             quantize_w1(t, t + 1)
-        round_w1(nc.vector.tensor_copy, 1, 0, P, 2, 4)
         quantize_w1(2, 4)
 
         h = [tile([P, S], F32, f"h{t}") for t in range(PACK)]
@@ -134,7 +137,7 @@ def tile_picked_sagecat_max_po_kernel(
 
         halves = [slice(a * HALF, (a + 1) * HALF) for a in range(2)]
         g = tile([P, PACK, V], BF16, "g")
-        nb = [reused.tile([P, PACK, V], BF16, name="nb0", align_bytes=64, offset=2 * PACK * V), tile([P, PACK, V], BF16, "nb1")]
+        nb = [reused.tile([P, PACK, V], BF16, name="nb0", align_bytes=64, offset=2 * PACK * V), tile([P, PACK, V], BF16, "nb1", tag="xg_w")]
         for piece in range(4):
             layer1(0, piece * P, (piece + 1) * P, 4 + piece)
         for t in range(1, PACK):

@@ -141,7 +141,8 @@ def tile_picked_sagecat_max_po_kernel(
         for piece in range(4):
             layer1(0, piece * P, (piece + 1) * P, 4 + piece)
         for t in range(1, PACK):
-            layer1(t, 0, S, t)
+            for a in range(2):
+                layer1(t, a * V, (a + 1) * V, 2 * (t - 1) + a)
         for t in range(PACK):
             vector_gather(g[:, t, :], h[t][:], cen_t[:])
         for t in range(PACK):

@@ -19,6 +19,7 @@ P = 128
 PACK = 4
 T, S, V, H = 1024, 512, 256, 512
 HALF = V // 2
+WINDOW_DISTANCE = 56 * 1024
 FLOPS = 2 * 512 * H * S + 2 * 2 * H * H * V
 
 
@@ -38,6 +39,7 @@ def tile_picked_sagecat_max_po_kernel(
         lists = ctx.enter_context(tc.tile_pool(name="lists", bufs=1))
         sb = ctx.enter_context(tc.tile_pool(name="sb", bufs=1))
         reused = ctx.enter_context(tc.tile_pool(name="reused", bufs=1))
+        far = ctx.enter_context(tc.tile_pool(name="far", bufs=1))
         psum = ctx.enter_context(tc.psum_pool(name="psum", bufs=1))
 
         def tile(shape, dtype, name, tag=None):
@@ -59,8 +61,8 @@ def tile_picked_sagecat_max_po_kernel(
         cen_t = lists.tile([P, V // 16], U16, name="cen_t")
         pos_t = [lists.tile([P, V // 16], U16, name=f"pos_t{d}") for d in range(3)]
 
-        xw = tile([P, T], I32, "xw")
-        xs = tile([P, T], U8, "xs")
+        xw = far.tile([P, T], I32, name="xw", align_bytes=64, offset=WINDOW_DISTANCE // 2)
+        xs = far.tile([P, T], U8, name="xs", align_bytes=64, offset=WINDOW_DISTANCE // 2 + 4 * T)
         ws = reused.tile([P, H], U8, name="ws", align_bytes=64, offset=2 * PACK * V - H // 2)
         w1_raw = [tile([P, 2, H], F32, f"w1_raw{u}") for u in range(2)]
         w2_raw = tile([P, H], I32, "w2_raw")
@@ -116,7 +118,7 @@ def tile_picked_sagecat_max_po_kernel(
             quantize_w1(t, t + 1)
         quantize_w1(2, 4)
 
-        h = [tile([P, S], F32, f"h{t}") for t in range(PACK)]
+        h = [far.tile([P, S], F32, name=f"h{t}", align_bytes=64, offset=t * WINDOW_DISTANCE) for t in range(PACK)]
 
         def layer1(t, lo, hi, bank):
             cols = slice(t * P, (t + 1) * P)

@@ -176,6 +176,7 @@ def tile_picked_sagecat_max_po_kernel(
         last.append(reused.tile([P, PACK, HALF], F32, name="last1", align_bytes=64, offset=0)[:])
         for t in range(PACK - 1):
             scalar_gather(last[1][:, t, :], h[t][:], pos_t[2][:, 8:16])
+        scalar_gather(last[1][:, PACK - 1, 64:HALF], h[PACK - 1][:], pos_t[2][:, 12:16])
         max01 = tile([P, PACK, V], BF16, "max01", tag="g")
         for cols in halves:
             nc.vector.tensor_tensor(max01[:, :, cols], nb[0][:, :, cols], nb[1][:, :, cols], MAX)
@@ -190,7 +191,7 @@ def tile_picked_sagecat_max_po_kernel(
                 MAX,
             )
             if a == 0:
-                vector_gather(last[1][:, PACK - 1, :], h[PACK - 1][:], pos_t[2][:, 8:16])
+                vector_gather(last[1][:, PACK - 1, 0:64], h[PACK - 1][:], pos_t[2][:, 8:12])
             quantize(z_q, z_s, halves[a], zi[:])
             passes(a, w3_d, 4, z_q, z_s, False)
 

@@ -27,10 +27,6 @@ def words_of(dram):
     return dram[0].rearrange("p n t -> p (n t)").bitcast(I32)
 
 
-def interleave(copy, dst, src):
-    copy(out=dst.rearrange("p (c i t) -> p c t i", i=4, t=PACK), in_=src.rearrange("p t (c i) -> p c t i", i=4))
-
-
 def tile_picked_sagecat_max_po_kernel(
     tc, x_words, x_scales, w1, w2_words, w2_scales, w3_words, w3_scales, offs, cen, pos1, pos2, pos3, out_0, out_1, out_2
 ):
@@ -139,7 +135,10 @@ def tile_picked_sagecat_max_po_kernel(
 
         halves = [slice(a * HALF, (a + 1) * HALF) for a in range(2)]
         g = tile([P, PACK, V], BF16, "g")
-        nb = [reused.tile([P, PACK, V], BF16, name="nb0", align_bytes=64, offset=2 * PACK * V), tile([P, PACK, V], BF16, "nb1", tag="xg_w")]
+        nb = [
+            reused.tile([P, 2, V, 2], BF16, name="nb0", align_bytes=64, offset=2 * PACK * V),
+            tile([P, 2, V, 2], BF16, "nb1", tag="xg_w"),
+        ]
         for piece in range(4):
             layer1(0, piece * P, (piece + 1) * P, 4 + piece)
         for t in range(1, PACK):
@@ -148,11 +147,11 @@ def tile_picked_sagecat_max_po_kernel(
         for t in range(PACK):
             vector_gather(g[:, t, :], h[t][:], cen_t[:])
         for t in range(PACK):
-            scalar_gather(nb[1][:, t, :], h[t][:], pos_t[1][:])
-            (vector_gather if t < PACK - 1 else scalar_gather)(nb[0][:, t, :], h[t][:], pos_t[0][:])
-        last = [tile([P, PACK, HALF], F32, "last0")[:]]
+            scalar_gather(nb[1][:, t // 2, :, t % 2], h[t][:], pos_t[1][:])
+            vector_gather(nb[0][:, t // 2, :, t % 2], h[t][:], pos_t[0][:])
+        last = [tile([P, 2, HALF, 2], BF16, "last0")]
         for t in range(PACK):
-            (scalar_gather if t < PACK - 1 else vector_gather)(last[0][:, t, :], h[t][:], pos_t[2][:, 0:8])
+            scalar_gather(last[0][:, t // 2, :, t % 2], h[t][:], pos_t[2][:, 0:8])
 
         z_q = tile([P, V], U32, "z_q")
         z_s = tile([P, V], U8, "z_s")
@@ -173,25 +172,28 @@ def tile_picked_sagecat_max_po_kernel(
             gi[:].rearrange("p (c t) -> p c t", t=PACK), g[:].rearrange("p t c -> p c t"), 1.0, 0.0, MULT, ADD
         )
         quantize(g_q, g_s, slice(0, V), gi[:])
-        last.append(reused.tile([P, PACK, HALF], F32, name="last1", align_bytes=64, offset=0)[:])
-        for t in range(PACK - 1):
-            scalar_gather(last[1][:, t, :], h[t][:], pos_t[2][:, 8:16])
-        scalar_gather(last[1][:, PACK - 1, 64:HALF], h[PACK - 1][:], pos_t[2][:, 12:16])
-        max01 = tile([P, PACK, V], BF16, "max01", tag="g")
+        last.append(reused.tile([P, 2, HALF, 2], BF16, name="last1", align_bytes=64, offset=0))
+        for t in range(2):
+            scalar_gather(last[1][:, 0, :, t], h[t][:], pos_t[2][:, 8:16])
+        for t in range(2, PACK):
+            scalar_gather(last[1][:, 1, 64:HALF, t - 2], h[t][:], pos_t[2][:, 12:16])
+        max01 = tile([P, 2, V, 2], BF16, "max01", tag="g")
         for cols in halves:
-            nc.vector.tensor_tensor(max01[:, :, cols], nb[0][:, :, cols], nb[1][:, :, cols], MAX)
+            nc.vector.tensor_tensor(max01[:, :, cols, :], nb[0][:, :, cols, :], nb[1][:, :, cols, :], MAX)
         for a in range(2):
             passes(a, w2_d, 0, g_q, g_s, True)
         for a in range(2):
             zi = tile([P, HALF * PACK], BF16, f"zi{a}")
+            if a == 0:
+                vector_gather(last[1][:, 1, 0:64, 0], h[2][:], pos_t[2][:, 8:12])
             nc.vector.tensor_tensor(
-                zi[:].rearrange("p (c i t) -> p c t i", i=4, t=PACK),
-                max01[:, :, halves[a]].rearrange("p t (c i) -> p c t i", i=4),
-                last[a].rearrange("p t (c i) -> p c t i", i=4),
+                zi[:].rearrange("p (c u e) -> p c u e", u=2, e=2),
+                max01[:, :, halves[a], :].rearrange("p u c e -> p c u e"),
+                last[a][:].rearrange("p u c e -> p c u e"),
                 MAX,
             )
             if a == 0:
-                vector_gather(last[1][:, PACK - 1, 0:64], h[PACK - 1][:], pos_t[2][:, 8:12])
+                vector_gather(last[1][:, 1, 0:64, 1], h[3][:], pos_t[2][:, 8:12])
             quantize(z_q, z_s, halves[a], zi[:])
             passes(a, w3_d, 4, z_q, z_s, False)
 

@@ -59,7 +59,7 @@ def tile_picked_sagecat_max_po_kernel(
 
         xw = far.tile([P, T], I32, name="xw", align_bytes=64, offset=WINDOW_DISTANCE // 2)
         xs = far.tile([P, T], U8, name="xs", align_bytes=64, offset=WINDOW_DISTANCE // 2 + 4 * T)
-        ws = reused.tile([P, H], U8, name="ws", align_bytes=64, offset=2 * PACK * V - H // 2)
+        ws = reused.tile([P, H], U8, name="ws", align_bytes=64, offset=0)
         w1_raw = [tile([P, 2, H], F32, f"w1_raw{u}") for u in range(2)]
         w2_raw = tile([P, H], I32, "w2_raw")
         w3_raw = tile([P, H], I32, "w3_raw")
@@ -77,13 +77,17 @@ def tile_picked_sagecat_max_po_kernel(
             scale_rows(nc.sync, xs, 0, x_scales, q)
         for u in range(2):
             nc.sync.dma_start(w1_raw[u][:], w1_pairs[u])
-        for list_tile, dram in zip(pos_t[:2] + [cen_t], (pos1, pos2, cen)):
-            nc.sync.dma_start(list_tile[:], dram)
-        nc.sync.dma_start(w2_raw[:], words_of(w2_words))
-        nc.sync.dma_start(w3_raw[:], words_of(w3_words))
+        nc.sync.dma_start(pos_t[0][:], pos1)
+        nc.sync.dma_start(pos_t[1][:], pos2)
+        nc.sync.dma_start(cen_t[:], cen)
+        for q in range(3):
+            scale_rows(nc.sync, ws, 0, w2_scales, q)
+        for raw, dram in ((w2_raw, w2_words), (w3_raw, w3_words)):
+            for cols in (slice(0, H // 2), slice(H // 2, H)):
+                nc.sync.dma_start(raw[:, cols], words_of(dram)[:, cols])
+        scale_rows(nc.sync, ws, 0, w2_scales, 3)
         for q in range(4):
             scale_rows(nc.sync, ws, 4, w3_scales, q)
-            scale_rows(nc.sync, ws, 0, w2_scales, q)
         nc.sync.dma_start(pos_t[2][:], pos3)
 
         xg_s = tile([P, S], U8, "xg_s")
@@ -128,30 +132,31 @@ def tile_picked_sagecat_max_po_kernel(
         ws_d = tile([P, H], U8, "ws_d")
         w_dealt = tile([P, 2, H], I32, "w_dealt", tag="w1_bf")
         w2_d, w3_d = w_dealt[:, 0, :], w_dealt[:, 1, :]
-        for dealt, raw in ((w2_d, w2_raw), (ws_d[:], ws), (w3_d, w3_raw)):
+        for dealt, raw in ((w2_d, w2_raw), (w3_d, w3_raw), (ws_d[:], ws)):
             nc.gpsimd.tensor_copy(
                 out=dealt.rearrange("p (t m) -> p t m", t=PACK), in_=raw[:].rearrange("p (m t) -> p t m", t=PACK)
             )
 
         halves = [slice(a * HALF, (a + 1) * HALF) for a in range(2)]
-        g = tile([P, PACK, V], BF16, "g")
-        nb = [
-            reused.tile([P, 2, V, 2], BF16, name="nb0", align_bytes=64, offset=2 * PACK * V),
-            tile([P, 2, V, 2], BF16, "nb1", tag="xg_w"),
-        ]
+        g = tile([P, PACK, V], BF16, "g", tag="xg_w")
+        nb = [tile([P, 2, V, 2], BF16, f"nb{d}") for d in range(2)]
+        last = [tile([P, 2, HALF, 2], BF16, f"last{a}") for a in range(2)]
         for piece in range(4):
             layer1(0, piece * P, (piece + 1) * P, 4 + piece)
         for t in range(1, PACK):
             for a in range(2):
                 layer1(t, a * V, (a + 1) * V, 2 * (t - 1) + a)
         for t in range(PACK):
-            vector_gather(g[:, t, :], h[t][:], cen_t[:])
-        for t in range(PACK):
-            scalar_gather(nb[1][:, t // 2, :, t % 2], h[t][:], pos_t[1][:])
-            vector_gather(nb[0][:, t // 2, :, t % 2], h[t][:], pos_t[0][:])
-        last = [tile([P, 2, HALF, 2], BF16, "last0")]
+            for d in range(2):
+                vector_gather(nb[d][:, t // 2, :, t % 2], h[t][:], pos_t[d][:])
+            scalar_gather(g[:, t, :], h[t][:], cen_t[:])
         for t in range(PACK):
             scalar_gather(last[0][:, t // 2, :, t % 2], h[t][:], pos_t[2][:, 0:8])
+        for t in range(2):
+            scalar_gather(last[1][:, 0, :, t], h[t][:], pos_t[2][:, 8:16])
+        for t in range(2, PACK):
+            scalar_gather(last[1][:, 1, 64:HALF, t - 2], h[t][:], pos_t[2][:, 12:16])
+            vector_gather(last[1][:, 1, 0:64, t - 2], h[t][:], pos_t[2][:, 8:12])
 
         z_q = tile([P, V], U32, "z_q")
         z_s = tile([P, V], U8, "z_s")
@@ -168,53 +173,63 @@ def tile_picked_sagecat_max_po_kernel(
                 )
 
         gi = reused.tile([P, V * PACK], BF16, name="gi", align_bytes=64, offset=0)
-        nc.gpsimd.tensor_scalar(
-            gi[:].rearrange("p (c t) -> p c t", t=PACK), g[:].rearrange("p t c -> p c t"), 1.0, 0.0, MULT, ADD
-        )
-        quantize(g_q, g_s, slice(0, V), gi[:])
-        last.append(reused.tile([P, 2, HALF, 2], BF16, name="last1", align_bytes=64, offset=0))
-        for t in range(2):
-            scalar_gather(last[1][:, 0, :, t], h[t][:], pos_t[2][:, 8:16])
-        for t in range(2, PACK):
-            scalar_gather(last[1][:, 1, 64:HALF, t - 2], h[t][:], pos_t[2][:, 12:16])
-        max01 = tile([P, 2, V, 2], BF16, "max01", tag="g")
-        for cols in halves:
+        for t0 in (0, 2):
+            gpsimd_copy(
+                gi[:].rearrange("p (c t) -> p c t", t=PACK)[:, :, t0 : t0 + 2],
+                g[:].rearrange("p t c -> p c t")[:, :, t0 : t0 + 2],
+            )
+        max01 = tile([P, 2, V, 2], BF16, "max01", tag="xg_w")
+        zi = [tile([P, HALF * PACK], BF16, f"zi{a}") for a in range(2)]
+
+        def first_max(a):
+            cols = halves[a]
             nc.vector.tensor_tensor(max01[:, :, cols, :], nb[0][:, :, cols, :], nb[1][:, :, cols, :], MAX)
-        for a in range(2):
-            passes(a, w2_d, 0, g_q, g_s, True)
-        for a in range(2):
-            zi = tile([P, HALF * PACK], BF16, f"zi{a}")
-            if a == 0:
-                vector_gather(last[1][:, 1, 0:64, 0], h[2][:], pos_t[2][:, 8:12])
+
+        def last_max(a):
             nc.vector.tensor_tensor(
-                zi[:].rearrange("p (c u e) -> p c u e", u=2, e=2),
+                zi[a][:].rearrange("p (c u e) -> p c u e", u=2, e=2),
                 max01[:, :, halves[a], :].rearrange("p u c e -> p c u e"),
                 last[a][:].rearrange("p u c e -> p c u e"),
                 MAX,
             )
-            if a == 0:
-                vector_gather(last[1][:, 1, 0:64, 1], h[3][:], pos_t[2][:, 8:12])
-            quantize(z_q, z_s, halves[a], zi[:])
-            passes(a, w3_d, 4, z_q, z_s, False)
 
-        o_q = tile([P, V], I32, "o_q")
+        first_max(0)
+        quantize(g_q, g_s, slice(0, V), gi[:])
+        for a in range(2):
+            passes(a, w2_d, 0, g_q, g_s, True)
+        last_max(0)
+        first_max(1)
+        quantize(z_q, z_s, halves[0], zi[0][:])
+        passes(0, w3_d, 4, z_q, z_s, False)
+        last_max(1)
+        quantize(z_q, z_s, halves[1], zi[1][:])
+        passes(1, w3_d, 4, z_q, z_s, False)
+
+        o_q = [tile([P, HALF], I32, "o_q0", tag="z_q"), tile([P, HALF], I32, "o_q1")]
         o_s = tile([P, V], U8, "o_s")
         out_rows = out_0.rearrange("(p t) v -> p t v", t=PACK)
+        y = [tile([P, PACK, HALF], F32, f"y{a}") for a in range(2)]
+        yi = [tile([P, HALF * PACK], BF16, f"yi{a}") for a in range(2)]
+
+        def interleave_y(a, t0, t1):
+            nc.vector.tensor_copy(
+                out=yi[a][:].rearrange("p (c i t) -> p c t i", i=4, t=PACK)[:, :, t0:t1, :],
+                in_=y[a][:].rearrange("p t (c i) -> p c t i", i=4)[:, :, t0:t1, :],
+            )
+
+        def quantize_y(a):
+            nc.vector.quantize_mx(out=o_q[a][:].bitcast(FP8X4), scales=o_s[:, halves[a]], in_=yi[a][:])
+            nc.sync.dma_start(words_of(out_1)[:, halves[a]], o_q[a][:])
+
         for a in range(2):
-            cols = halves[a]
-            y = tile([P, PACK, HALF], F32, f"y{a}")
-            yi = tile([P, HALF * PACK], BF16, f"yi{a}")
             for t in range(PACK):
-                nc.scalar.copy(y[:, t, :], acc[a][t][:])
-            nc.sync.dma_start(out_rows[:, :, cols], y[:])
-            pieces = ((0, 4),) if a == 0 else ((0, 2), (2, 4))
-            for t0, t1 in pieces:
-                nc.vector.tensor_copy(
-                    out=yi[:].rearrange("p (c i t) -> p c t i", i=4, t=PACK)[:, :, t0:t1, :],
-                    in_=y[:].rearrange("p t (c i) -> p c t i", i=4)[:, :, t0:t1, :],
-                )
-            quantize(o_q, o_s, cols, yi[:])
-            nc.sync.dma_start(words_of(out_1)[:, cols], o_q[:, cols])
+                nc.scalar.copy(y[a][:, t, :], acc[a][t][:])
+            nc.sync.dma_start(out_rows[:, :, halves[a]], y[a][:])
+        interleave_y(0, 0, 4)
+        interleave_y(1, 0, 2)
+        quantize_y(0)
+        interleave_y(1, 2, 4)
+        quantize_y(1)
         for q in range(4):
             queue = nc.scalar if q == 3 else nc.sync
             queue.dma_start(out_2[0, 4 * q : 4 * q + 4, :].bitcast(I32), o_s[32 * q : 32 * q + 4, :].bitcast(I32))

@@ -162,14 +162,18 @@ def tile_picked_sagecat_max_po_kernel(
         z_s = tile([P, V], U8, "z_s")
         g_q = tile([P, V], U32, "g_q")
         g_s = tile([P, V], U8, "g_s")
-        acc = [[psum.tile([P, HALF], F32, name=f"acc{a}{t}", tag=f"bank{4 * (1 - a) + t}") for t in range(PACK)] for a in range(2)]
+        acc_pair = psum.tile([P, 2, HALF], F32, name="acc_pair", tag="bank2")
+        acc = [
+            [psum.tile([P, HALF], F32, name=f"acc0{t}", tag=f"bank{4 + t}")[:] for t in range(PACK)],
+            [psum.tile([P, HALF], F32, name=f"acc1{t}", tag=f"bank{t}")[:] for t in range(2)] + [acc_pair[:, e, :] for e in range(2)],
+        ]
 
         def passes(a, w_d, plane, codes, scales, first):
             for t in range(PACK):
                 m = slice(t * P, (t + 1) * P)
                 nc.tensor.matmul_mx(
-                    out=acc[a][t][:], lhsT=w_d[:, m].bitcast(FP8X4), lhsT_scale=ws_d[plane:P, m],
-                    rhs=codes[:, halves[a]].bitcast(FP8X4), rhs_scale=scales[:, halves[a]], start=first, stop=not first,
+                    out=acc[a][t], lhsT=w_d[:, m].bitcast(FP8X4), lhsT_scale=ws_d[plane:P, m],
+                    rhs=codes[:, halves[a]].bitcast(FP8X4), rhs_scale=scales[:, halves[a]], start=first and (a, t) != (1, 3), stop=not first and (a, t) != (1, 2),
                 )
 
         gi = reused.tile([P, V * PACK], BF16, name="gi", align_bytes=64, offset=0)
@@ -205,7 +209,7 @@ def tile_picked_sagecat_max_po_kernel(
         quantize(z_q, z_s, halves[1], zi[1][:])
         passes(1, w3_d, 4, z_q, z_s, False)
 
-        o_q = [tile([P, HALF], I32, "o_q0", tag="z_q"), tile([P, HALF], I32, "o_q1")]
+        o_q = tile([P, V], I32, "o_q", tag="z_q")
         o_s = tile([P, V], U8, "o_s")
         out_rows = out_0.rearrange("(p t) v -> p t v", t=PACK)
         y = [tile([P, PACK, HALF], F32, f"y{a}") for a in range(2)]
@@ -218,18 +222,24 @@ def tile_picked_sagecat_max_po_kernel(
             )
 
         def quantize_y(a):
-            nc.vector.quantize_mx(out=o_q[a][:].bitcast(FP8X4), scales=o_s[:, halves[a]], in_=yi[a][:])
-            nc.sync.dma_start(words_of(out_1)[:, halves[a]], o_q[a][:])
+            nc.vector.quantize_mx(out=o_q[:, halves[a]].bitcast(FP8X4), scales=o_s[:, halves[a]], in_=yi[a][:])
 
-        for a in range(2):
-            for t in range(PACK):
-                nc.scalar.copy(y[a][:, t, :], acc[a][t][:])
-            nc.sync.dma_start(out_rows[:, :, halves[a]], y[a][:])
+        for t in range(PACK):
+            nc.scalar.copy(y[0][:, t, :], acc[0][t])
+        nc.sync.dma_start(out_rows[:, :, halves[0]], y[0][:])
+        for t in range(2):
+            nc.scalar.copy(y[1][:, t, :], acc[1][t])
+        nc.sync.dma_start(out_rows[:, 0:2, halves[1]], y[1][:, 0:2, :])
+        nc.scalar.copy(
+            yi[1][:].rearrange("p (c t) -> p c t", t=PACK)[:, :, 2:4], acc_pair[:].rearrange("p e c -> p c e")
+        )
+        nc.scalar.copy(y[1][:, 2:4, :], acc_pair[:])
+        nc.sync.dma_start(out_rows[:, 2:4, halves[1]], y[1][:, 2:4, :])
         interleave_y(0, 0, 4)
         interleave_y(1, 0, 2)
         quantize_y(0)
-        interleave_y(1, 2, 4)
         quantize_y(1)
+        nc.sync.dma_start(words_of(out_1), o_q[:])
         for q in range(4):
             queue = nc.scalar if q == 3 else nc.sync
             queue.dma_start(out_2[0, 4 * q : 4 * q + 4, :].bitcast(I32), o_s[32 * q : 32 * q + 4, :].bitcast(I32))

from contextlib import ExitStack

import concourse.mybir as mybir

F32 = mybir.dt.float32
BF16 = mybir.dt.bfloat16
I32 = mybir.dt.int32
U32 = mybir.dt.uint32
U16 = mybir.dt.uint16
U8 = mybir.dt.uint8
FP8X4 = mybir.dt.float8_e4m3fn_x4
COPY = mybir.ActivationFunctionType.Copy
RELU = mybir.ActivationFunctionType.Relu
MAX = mybir.AluOpType.max
MULT = mybir.AluOpType.mult
ADD = mybir.AluOpType.add

P = 128
PACK = 4
T, S, V, H = 1024, 512, 256, 512
HALF = V // 2
WINDOW_DISTANCE = 56 * 1024
FLOPS = 2 * 512 * H * S + 2 * 2 * H * H * V


def words_of(dram):
    return dram[0].rearrange("p n t -> p (n t)").bitcast(I32)


def tile_picked_sagecat_max_po_kernel(
    tc, x_words, x_scales, w1, w2_words, w2_scales, w3_words, w3_scales, offs, cen, pos1, pos2, pos3, out_0, out_1, out_2
):
    nc = tc.nc
    with ExitStack() as ctx:
        lists = ctx.enter_context(tc.tile_pool(name="lists", bufs=1))
        sb = ctx.enter_context(tc.tile_pool(name="sb", bufs=1))
        reused = ctx.enter_context(tc.tile_pool(name="reused", bufs=1))
        far = ctx.enter_context(tc.tile_pool(name="far", bufs=1))
        psum = ctx.enter_context(tc.psum_pool(name="psum", bufs=1))

        def tile(shape, dtype, name, tag=None):
            return sb.tile(shape, dtype, name=name, tag=tag or name, align_bytes=64)

        def quantize(codes, scales, cols, src):
            nc.vector.quantize_mx(out=codes[:, cols].bitcast(FP8X4), scales=scales[:, cols], in_=src)

        def vector_gather(out, window, offsets):
            nc.vector.tensor_copy(out, window.indirect(offsets))

        def scalar_gather(out, window, offsets):
            nc.scalar.activation(out, window.indirect(offsets), COPY)

        def gpsimd_copy(out, in_):
            nc.gpsimd.tensor_scalar(out, in_, 1.0, 0.0, MULT, ADD)

        offs_t = lists.tile([P, S // 16], U16, name="offs_t")
        cen_t = lists.tile([P, V // 16], U16, name="cen_t")
        pos_t = [lists.tile([P, V // 16], U16, name=f"pos_t{d}") for d in range(3)]

        xw = far.tile([P, T], I32, name="xw", align_bytes=64, offset=WINDOW_DISTANCE // 2)
        xs = far.tile([P, T], U8, name="xs", align_bytes=64, offset=WINDOW_DISTANCE // 2 + 4 * T)
        ws = reused.tile([P, H], U8, name="ws", align_bytes=64, offset=0)
        w1_raw = [tile([P, 2, H], F32, f"w1_raw{u}") for u in range(2)]
        w2_raw = tile([P, H], I32, "w2_raw")
        w3_raw = tile([P, H], I32, "w3_raw")

        nc.gpsimd.memset(xs[:].bitcast(I32), 0)
        nc.vector.memset(ws[:].bitcast(I32), 0)

        def scale_rows(queue, dst, first, dram, q):
            queue.dma_start(dst[32 * q + first : 32 * q + first + 4, :].bitcast(I32), dram[0, 4 * q : 4 * q + 4, :].bitcast(I32))

        w1_pairs = w1.rearrange("(p u e) c -> u p e c", u=2, e=2)
        nc.sync.dma_start(xw[:], words_of(x_words))
        nc.sync.dma_start(offs_t[:], offs)
        for q in range(4):
            scale_rows(nc.sync, xs, 0, x_scales, q)
        for u in range(2):
            nc.sync.dma_start(w1_raw[u][:], w1_pairs[u])
        nc.sync.dma_start(pos_t[0][:], pos1)
        nc.sync.dma_start(pos_t[1][:], pos2)
        nc.sync.dma_start(cen_t[:], cen)
        for q in range(3):
            scale_rows(nc.sync, ws, 0, w2_scales, q)
        for raw, dram in ((w2_raw, w2_words), (w3_raw, w3_words)):
            for cols in (slice(0, H // 2), slice(H // 2, H)):
                nc.sync.dma_start(raw[:, cols], words_of(dram)[:, cols])
        scale_rows(nc.sync, ws, 0, w2_scales, 3)
        for q in range(4):
            scale_rows(nc.sync, ws, 4, w3_scales, q)
        nc.sync.dma_start(pos_t[2][:], pos3)

        xg_s = tile([P, S], U8, "xg_s")
        xg_w = tile([P, S], I32, "xg_w")
        vector_gather(xg_w[:].bitcast(U32), xw[:].bitcast(U32), offs_t[:])
        vector_gather(xg_s[:], xs[:], offs_t[:])

        w1_bf = tile([P, PACK * P * PACK], BF16, "w1_bf")
        w1_q = tile([P, H], U32, "w1_q")
        w1_s = tile([P, H], U8, "w1_s")

        def round_w1(copy, u, m0, m1, t0, t1):
            copy(
                out=w1_bf[:].rearrange("p (t m u e) -> p u m t e", t=PACK, u=2, e=2)[:, u, m0:m1, t0:t1, :],
                in_=w1_raw[u][:].rearrange("p e (m t) -> p m t e", t=PACK)[:, m0:m1, t0:t1, :],
            )

        def quantize_w1(t0, t1):
            quantize(w1_q, w1_s, slice(t0 * P, t1 * P), w1_bf[:, t0 * P * PACK : t1 * P * PACK])

        round_w1(lambda out, in_: nc.scalar.activation(out, in_, COPY), 0, 0, 4, 0, 2)
        round_w1(nc.scalar.copy, 0, 4, P, 0, 2)
        round_w1(gpsimd_copy, 0, 0, P, 2, 4)
        round_w1(nc.scalar.copy, 1, 0, P // 2, 0, 2)
        round_w1(gpsimd_copy, 1, P // 2, P, 0, 2)
        round_w1(nc.scalar.copy, 1, 0, P, 2, 4)
        for t in range(2):
            quantize_w1(t, t + 1)
        quantize_w1(2, 4)

        h = [far.tile([P, S], F32, name=f"h{t}", align_bytes=64, offset=t * WINDOW_DISTANCE) for t in range(PACK)]

        def layer1(t, lo, hi, bank):
            cols = slice(t * P, (t + 1) * P)
            acc = psum.tile([P, hi - lo], F32, name=f"acc_h{t}_{lo}", tag=f"bank{bank}")
            nc.tensor.matmul_mx(
                out=acc[:], lhsT=w1_q[:, cols].bitcast(FP8X4), lhsT_scale=w1_s[:, cols],
                rhs=xg_w[:, lo:hi].bitcast(FP8X4), rhs_scale=xg_s[:, lo:hi], start=True, stop=True,
            )
            nc.scalar.activation(h[t][:, lo:hi], acc[:], RELU)

        ws_d = tile([P, H], U8, "ws_d")
        w_dealt = tile([P, 2, H], I32, "w_dealt", tag="w1_bf")
        w2_d, w3_d = w_dealt[:, 0, :], w_dealt[:, 1, :]
        for dealt, raw in ((w2_d, w2_raw), (w3_d, w3_raw), (ws_d[:], ws)):
            nc.gpsimd.tensor_copy(
                out=dealt.rearrange("p (t m) -> p t m", t=PACK), in_=raw[:].rearrange("p (m t) -> p t m", t=PACK)
            )

        halves = [slice(a * HALF, (a + 1) * HALF) for a in range(2)]
        g = tile([P, PACK, V], BF16, "g", tag="xg_w")
        nb = [tile([P, 2, V, 2], BF16, f"nb{d}") for d in range(2)]
        last = [tile([P, 2, HALF, 2], BF16, f"last{a}") for a in range(2)]
        for piece in range(4):
            layer1(0, piece * P, (piece + 1) * P, 4 + piece)
        for t in range(1, PACK):
            for a in range(2):
                layer1(t, a * V, (a + 1) * V, 2 * (t - 1) + a)
        for t in range(PACK):
            for d in range(2):
                vector_gather(nb[d][:, t // 2, :, t % 2], h[t][:], pos_t[d][:])
            scalar_gather(g[:, t, :], h[t][:], cen_t[:])
        for t in range(PACK):
            scalar_gather(last[0][:, t // 2, :, t % 2], h[t][:], pos_t[2][:, 0:8])
        for t in range(2):
            scalar_gather(last[1][:, 0, :, t], h[t][:], pos_t[2][:, 8:16])
        for t in range(2, PACK):
            scalar_gather(last[1][:, 1, 64:HALF, t - 2], h[t][:], pos_t[2][:, 12:16])
            vector_gather(last[1][:, 1, 0:64, t - 2], h[t][:], pos_t[2][:, 8:12])

        z_q = tile([P, V], U32, "z_q")
        z_s = tile([P, V], U8, "z_s")
        g_q = tile([P, V], U32, "g_q")
        g_s = tile([P, V], U8, "g_s")
        acc_pair = psum.tile([P, 2, HALF], F32, name="acc_pair", tag="bank2")
        acc = [
            [psum.tile([P, HALF], F32, name=f"acc0{t}", tag=f"bank{4 + t}")[:] for t in range(PACK)],
            [psum.tile([P, HALF], F32, name=f"acc1{t}", tag=f"bank{t}")[:] for t in range(2)] + [acc_pair[:, e, :] for e in range(2)],
        ]

        def passes(a, w_d, plane, codes, scales, first):
            for t in range(PACK):
                m = slice(t * P, (t + 1) * P)
                nc.tensor.matmul_mx(
                    out=acc[a][t], lhsT=w_d[:, m].bitcast(FP8X4), lhsT_scale=ws_d[plane:P, m],
                    rhs=codes[:, halves[a]].bitcast(FP8X4), rhs_scale=scales[:, halves[a]], start=first and (a, t) != (1, 3), stop=not first and (a, t) != (1, 2),
                )

        gi = reused.tile([P, V * PACK], BF16, name="gi", align_bytes=64, offset=0)
        for t0 in (0, 2):
            gpsimd_copy(
                gi[:].rearrange("p (c t) -> p c t", t=PACK)[:, :, t0 : t0 + 2],
                g[:].rearrange("p t c -> p c t")[:, :, t0 : t0 + 2],
            )
        max01 = tile([P, 2, V, 2], BF16, "max01", tag="xg_w")
        zi = [tile([P, HALF * PACK], BF16, f"zi{a}") for a in range(2)]

        def first_max(a):
            cols = halves[a]
            nc.vector.tensor_tensor(max01[:, :, cols, :], nb[0][:, :, cols, :], nb[1][:, :, cols, :], MAX)

        def last_max(a):
            nc.vector.tensor_tensor(
                zi[a][:].rearrange("p (c u e) -> p c u e", u=2, e=2),
                max01[:, :, halves[a], :].rearrange("p u c e -> p c u e"),
                last[a][:].rearrange("p u c e -> p c u e"),
                MAX,
            )

        first_max(0)
        quantize(g_q, g_s, slice(0, V), gi[:])
        for a in range(2):
            passes(a, w2_d, 0, g_q, g_s, True)
        last_max(0)
        first_max(1)
        quantize(z_q, z_s, halves[0], zi[0][:])
        passes(0, w3_d, 4, z_q, z_s, False)
        last_max(1)
        quantize(z_q, z_s, halves[1], zi[1][:])
        passes(1, w3_d, 4, z_q, z_s, False)

        o_q = tile([P, V], I32, "o_q", tag="z_q")
        o_s = tile([P, V], U8, "o_s")
        out_rows = out_0.rearrange("(p t) v -> p t v", t=PACK)
        y = [tile([P, PACK, HALF], F32, f"y{a}") for a in range(2)]
        yi = [tile([P, HALF * PACK], BF16, f"yi{a}") for a in range(2)]

        def interleave_y(a, t0, t1):
            nc.vector.tensor_copy(
                out=yi[a][:].rearrange("p (c i t) -> p c t i", i=4, t=PACK)[:, :, t0:t1, :],
                in_=y[a][:].rearrange("p t (c i) -> p c t i", i=4)[:, :, t0:t1, :],
            )

        def quantize_y(a):
            nc.vector.quantize_mx(out=o_q[:, halves[a]].bitcast(FP8X4), scales=o_s[:, halves[a]], in_=yi[a][:])

        for t in range(PACK):
            nc.scalar.copy(y[0][:, t, :], acc[0][t])
        nc.sync.dma_start(out_rows[:, :, halves[0]], y[0][:])
        for t in range(2):
            nc.scalar.copy(y[1][:, t, :], acc[1][t])
        nc.sync.dma_start(out_rows[:, 0:2, halves[1]], y[1][:, 0:2, :])
        nc.scalar.copy(
            yi[1][:].rearrange("p (c t) -> p c t", t=PACK)[:, :, 2:4], acc_pair[:].rearrange("p e c -> p c e")
        )
        nc.scalar.copy(y[1][:, 2:4, :], acc_pair[:])
        nc.sync.dma_start(out_rows[:, 2:4, halves[1]], y[1][:, 2:4, :])
        interleave_y(0, 0, 4)
        interleave_y(1, 0, 2)
        quantize_y(0)
        quantize_y(1)
        nc.sync.dma_start(words_of(out_1), o_q[:])
        for q in range(4):
            queue = nc.scalar if q == 3 else nc.sync
            queue.dma_start(out_2[0, 4 * q : 4 * q + 4, :].bitcast(I32), o_s[32 * q : 32 * q + 4, :].bitcast(I32))
